import numpy as np
import ml_dtypes


def mxq(x, axis, fmt="e4m3"):
    dtype, down = {"e4m3": (ml_dtypes.float8_e4m3fn, 7), "e5m2": (ml_dtypes.float8_e5m2, 14)}[fmt]
    v = np.moveaxis(np.asarray(x, np.float32).astype(ml_dtypes.bfloat16).astype(np.float64), axis, -1)
    blocks = v.reshape(v.shape[:-1] + (-1, 32))
    amax = np.abs(blocks).max(-1, keepdims=True)
    byte = np.maximum(np.where(amax > 0, np.frexp(amax)[1] - 1 + 127, 0) - down, 1)
    scale = np.exp2(byte - 127.0)
    codes = (blocks / scale).astype(np.float32).astype(dtype).astype(np.float64)
    return np.moveaxis((codes * scale).reshape(v.shape), -1, axis)


WIDE = False


def mx_kscale(k):
    if not WIDE:
        return np.ones(k)
    levels = np.array([10, -10, 5, -5, 0])
    if k % 512:
        return np.exp2(np.random.permutation(np.resize(levels, k // 32))).repeat(32)
    a = np.empty((k // 512, 16))
    for p in range(k // 512):
        a[p, :8] = np.random.permutation(np.resize(levels, 8))
        for g in range(8):
            far = levels[np.abs(levels - a[p, g]) >= 10]
            a[p, g + 8] = far[np.random.randint(len(far))]
    return np.exp2(a.ravel()).repeat(32)


BF16 = ml_dtypes.bfloat16


def bf(x):
    return np.asarray(x, np.float32).astype(BF16)


def f64(x):
    return np.asarray(x).astype(np.float64)


H, L, D, N = 4, 1024, 1024, 1024


def softplus(a):
    return np.maximum(a, 0.0) + np.log(1.0 + np.exp(-np.abs(a)))


def setup_inputs():
    s = mx_kscale(D)
    t = mx_kscale(L)
    return {"x": bf(np.random.standard_normal((L, D)) * s),
            "w_in": bf(np.random.standard_normal((D, N)) / np.sqrt(D) / s[:, None]),
            "w_step": bf(np.random.standard_normal((D, N)) / np.sqrt(D) / s[:, None]),
            "b_step": bf(0.5 * np.random.standard_normal(N)),
            "tau": bf(np.exp(0.3 * np.random.standard_normal(L)) * t),
            "kernel": bf(np.random.standard_normal((H, L, L)) / np.sqrt(L) / t),
            "alpha": bf(np.random.uniform(0.2, 1.0, (H, L))),
            "h0": bf(np.random.standard_normal(N)),
            "d": bf(1.0 + 0.1 * np.random.standard_normal(N))}


def reference(x, w_in, w_step, b_step, tau, kernel, alpha, h0, d):
    xq = mxq(f64(x), 1, "e4m3")
    v = xq @ mxq(f64(w_in), 0, "e4m3")
    g = (xq @ mxq(f64(w_step), 0, "e4m3")) + f64(b_step)
    u = f64(tau)[:, None] * softplus(g) * v
    uq = mxq(u, 0, "e4m3").reshape(L, H, N // H).transpose(1, 0, 2)
    h = mxq(f64(kernel), 2, "e4m3") @ uq
    h = h + f64(alpha)[:, :, None] * f64(h0).reshape(H, 1, N // H)
    return h.transpose(1, 0, 2).reshape(L, N) + f64(d) * v

@@ -1,0 +1,579 @@
+from contextlib import ExitStack
+
+import concourse.mybir as mybir
+from concourse.masks import make_identity
+
+H, L, D, N = 4, 1024, 1024, 1024
+C = N // H
+FLOPS = 2 * 2 * L * D * N + 2 * H * L * L * C
+
+F32 = mybir.dt.float32
+BF16 = mybir.dt.bfloat16
+U32 = mybir.dt.uint32
+U8 = mybir.dt.uint8
+FP8X4 = mybir.dt.float8_e4m3fn_x4
+ACT = mybir.ActivationFunctionType
+ALU = mybir.AluOpType
+
+P = 128
+PACK = 4
+K_PASS = P * PACK
+TINY = 2.0**-63
+
+
+def tile_step_weighted_time_kernel_f4_kernel(
+    tc, x, w_in, w_step, b_step, tau, kernel, alpha, h0, d, out
+):
+    nc = tc.nc
+
+    with ExitStack() as ctx:
+        raw_pool = ctx.enter_context(tc.tile_pool(name="raw", bufs=11))
+        grp_pool = ctx.enter_context(tc.tile_pool(name="grp", bufs=5))
+        keep = ctx.enter_context(tc.tile_pool(name="keep", bufs=1))
+        kc_pool = ctx.enter_context(tc.tile_pool(name="kc", bufs=12))
+        uc_pool = ctx.enter_context(tc.tile_pool(name="uc", bufs=8))
+        ub_pool = ctx.enter_context(tc.tile_pool(name="ub", bufs=3))
+        tr_psum = ctx.enter_context(tc.psum_pool(name="tr", bufs=3))
+        acc_psum = ctx.enter_context(tc.psum_pool(name="acc", bufs=3))
+        h_psum = ctx.enter_context(tc.psum_pool(name="hp", bufs=2))
+        ctx.enter_context(tc.manual_schedule())
+
+        dummy = keep.tile([P, 1], F32, name="dummy")
+        nc.vector.memset(dummy[:], 0.0)
+        nc.scalar.activation(out=dummy[:], in_=dummy[:], func=ACT.Sigmoid)
+        rows = keep.tile([P, K_PASS], BF16, name="rows")
+        vecs = keep.tile([P, N], BF16, name="vecs")
+        nc.vector.memset(rows[:], 0.0)
+        nc.vector.memset(vecs[:], 0.0)
+        ident = keep.tile([P, P], F32, name="ident")
+        make_identity(nc, ident[:])
+        ident_b = keep.tile([P, P], BF16, name="ident_b")
+        nc.vector.tensor_copy(out=ident_b[:], in_=ident[:])
+        nc.scalar.dma_start(out=vecs[0:1, :], in_=b_step.unsqueeze(0))
+        nc.scalar.dma_start(out=vecs[1:2, :], in_=h0.unsqueeze(0))
+        nc.scalar.dma_start(out=vecs[2:3, :], in_=d.unsqueeze(0))
+        nc.scalar.dma_start(out=rows[0:8, :], in_=alpha.rearrange("h (g q) -> (h g) q", q=K_PASS))
+        nc.scalar.dma_start(out=rows[8:10, :], in_=tau.rearrange("(g q) -> g q", q=K_PASS))
+
+        def load_rows(src, g, half):
+            raw = raw_pool.tile([P, 2, 1024], BF16, name="raw", align_bytes=64)
+            view = src[g * K_PASS : (g + 1) * K_PASS, :].rearrange("(m t) k -> m t k", t=PACK)
+            nc.sync.dma_start(out=raw[:], in_=view[:, 2 * half : 2 * half + 2, :])
+            return raw
+
+        def load_w(w, nh, kp):
+            raw = raw_pool.tile([P, PACK, 512], BF16, name="raw", align_bytes=64)
+            view = w[kp * K_PASS : (kp + 1) * K_PASS, nh * 512 : (nh + 1) * 512]
+            nc.sync.dma_start(out=raw[:], in_=view.rearrange("(p j) n -> p j n", j=PACK))
+            return raw
+
+        def copy(eng, out_ap, in_ap):
+            if eng == "s":
+                nc.scalar.copy(out_ap, in_ap)
+            elif eng == "v":
+                nc.vector.tensor_copy(out=out_ap, in_=in_ap)
+            else:
+                nc.gpsimd.tensor_scalar(
+                    out=out_ap, in0=in_ap, scalar1=1.0, scalar2=0.0, op0=ALU.mult, op1=ALU.add
+                )
+
+        def new_groups():
+            pair = []
+            for kp in range(2):
+                grp = grp_pool.tile([P, 2048], BF16, name="grp", align_bytes=64)
+                pair.append(grp)
+            return pair
+
+        def turn(raw, half, groups, engs):
+            words = raw[:].rearrange("p t k -> p (t k)").bitcast(F32)
+            for kp in range(2):
+                bank = tr_psum.tile([P, 2, 2, P], F32, name="bank")
+                for tt in range(2):
+                    for u in range(2):
+                        first = tt * 512 + 256 * kp + u
+                        nc.tensor.transpose(
+                            bank[:, tt, u, :], words[:, first : tt * 512 + 256 * (kp + 1) : 2], ident[:]
+                        )
+                dst = groups[kp][:].bitcast(F32)[:, 512 * half : 512 * (half + 1)]
+                copy(
+                    engs[kp],
+                    dst.rearrange("p (t r u) -> p t r u", t=2, u=2),
+                    bank[:].rearrange("p t u r -> p t r u"),
+                )
+
+        def quantize(grp, pool, name):
+            width = grp.shape[1] // PACK
+            codes = pool.tile([P, width], U32, name=name + "_c", align_bytes=64)
+            scales = pool.tile([P, width], U8, name=name + "_s", align_bytes=64)
+            nc.vector.quantize_mx(out=codes[:].bitcast(FP8X4), scales=scales[:], in_=grp[:])
+            return codes, scales
+
+        def interleave(eng, grp, raw, width):
+            copy(
+                eng,
+                grp[:].rearrange("p (c i t) -> p c t i", i=4, t=PACK),
+                raw[:].rearrange("p t (c i) -> p c t i", i=4),
+            )
+
+        def prep_w(raw, eng, name):
+            grp = grp_pool.tile([P, 2048], BF16, name="grp", align_bytes=64)
+            interleave(eng, grp, raw, 512)
+            return quantize(grp, keep, name)
+
+        def mx(out_ap, stat, c0, mov, n0, width, start, stop):
+            nc.tensor.matmul_mx(
+                out=out_ap,
+                lhsT=stat[0][:, c0 : c0 + P].bitcast(FP8X4),
+                lhsT_scale=stat[1][:, c0 : c0 + P],
+                rhs=mov[0][:, n0 : n0 + width].bitcast(FP8X4),
+                rhs_scale=mov[1][:, n0 : n0 + width],
+                start=start,
+                stop=stop,
+            )
+
+        rx = {}
+        rw = {}
+        rk = {}
+
+        def load_x(g):
+            for half in range(2):
+                rx[g, half] = load_rows(x, g, half)
+
+        def load_ws(w, tag, nh):
+            for kp in range(2):
+                rw[tag, nh, kp] = load_w(w, nh, kp)
+
+        def load_one_x(g, half):
+            rx[g, half] = load_rows(x, g, half)
+
+        def load_one_w(w, tag, nh, kp):
+            rw[tag, nh, kp] = load_w(w, nh, kp)
+
+        def load_k(j):
+            for g in range(2):
+                for half in range(2):
+                    rk[j, g, half] = load_rows(kernel[j], g, half)
+
+        sm = keep.tile([P, PACK, 10], F32, name="sm")
+        bc = keep.tile([P, 3, N], BF16, name="bc")
+
+        def prep_cols():
+            bank = tr_psum.tile([P, PACK, P], BF16, name="bank")
+            for t in range(PACK):
+                nc.tensor.transpose(bank[:, t, :], rows[:, t : K_PASS : PACK], ident_b[:])
+            nc.vector.tensor_copy(out=sm[:], in_=bank[:, :, 0:10])
+
+        def spread(r, eng):
+            bank = acc_psum.tile([P, N], BF16, name="acc")
+            for nh in range(2):
+                nc.tensor.matmul(
+                    bank[:, nh * 512 : (nh + 1) * 512],
+                    lhsT=ident_b[:, r : r + 1].to_broadcast([P, P]),
+                    rhs=vecs[:, nh * 512 : (nh + 1) * 512],
+                    start=True,
+                    stop=True,
+                )
+            copy(eng, bc[:, r, :], bank[:])
+
+        qx = {}
+        qw = {}
+        qk = {}
+        qu = {}
+        a = {}
+        sg = {}
+        for lg in range(2):
+            for nh in range(2):
+                a[lg, nh] = keep.tile([P, PACK, 512], F32, name="a%d%d" % (lg, nh))
+                sg[lg, nh] = keep.tile([P, PACK, 512], F32, name="sg%d%d" % (lg, nh))
+
+        def prep_x(g, engs):
+            groups = new_groups()
+            for half in range(2):
+                turn(rx[g, half], half, groups, engs)
+            for kp in range(2):
+                qx[g, kp] = quantize(groups[kp], keep, "qx%d%d" % (g, kp))
+
+        def prep_k(j, g, engs):
+            groups = new_groups()
+            for half in range(2):
+                turn(rk[j, g, half], half, groups, engs)
+            for kp in range(2):
+                qk[j, g, kp] = quantize(groups[kp], kc_pool, "qk")
+
+        def g_mm(lg, nh, t):
+            acc = acc_psum.tile([P, 512], F32, name="acc")
+            for kp in range(2):
+                mx(acc[:], qx[lg, kp], t * P, qw["s", nh, kp], 0, 512, kp == 0, kp == 1)
+            gacc[lg, nh, t] = acc
+
+        def g_use(lg, nh, t):
+            acc = gacc[lg, nh, t]
+            nc.vector.tensor_tensor(
+                out=a[lg, nh][:, t, :], in0=acc[:], in1=bc[:, 0, nh * 512 : (nh + 1) * 512], op=ALU.add
+            )
+
+        def sig(lg, nh, tp):
+            pair = slice(2 * tp, 2 * tp + 2)
+            nc.scalar.activation(
+                out=sg[lg, nh][:, pair, :], in_=a[lg, nh][:, pair, :], func=ACT.Sigmoid, scale=-1.0
+            )
+
+        def cols_of(j):
+            return slice((j % 2) * C, (j % 2 + 1) * C)
+
+        def ln(j, lg):
+            s = sg[lg, j // 2][:, :, cols_of(j)]
+            nc.scalar.activation(out=s, in_=s, func=ACT.Ln, bias=TINY)
+
+        def m_max(j, lg):
+            m = sg[lg, j // 2][:, :, cols_of(j)]
+            av = a[lg, j // 2][:, :, cols_of(j)]
+            nc.vector.scalar_tensor_tensor(out=m, in0=m, scalar=-1.0, in1=av, op0=ALU.mult, op1=ALU.max)
+
+        vacc = {}
+        gacc = {}
+        ub_of = {}
+        ug_of = {}
+        hacc = {}
+
+        def v_mm(j, lg, tp):
+            acc = acc_psum.tile([P, 2, C], F32, name="acc")
+            for tt in range(2):
+                for kp in range(2):
+                    mx(acc[:, tt, :], qx[lg, kp], (2 * tp + tt) * P, qw["i", j // 2, kp], (j % 2) * C, C, kp == 0, kp == 1)
+            vacc[j, lg, tp] = acc
+
+        def v_use(j, lg, tp):
+            acc = vacc[j, lg, tp]
+            m = sg[lg, j // 2][:, :, cols_of(j)]
+            av = a[lg, j // 2][:, :, cols_of(j)]
+            if (j, lg) not in ub_of:
+                ub = ub_pool.tile([P, PACK, C], BF16, name="ub", align_bytes=64)
+                ub_of[j, lg] = ub
+            for tt in range(2):
+                t = 2 * tp + tt
+                nc.vector.scalar_tensor_tensor(
+                    out=ub_of[j, lg][:, t, :],
+                    in0=m[:, t, :],
+                    scalar=sm[:, t, 8 + lg : 9 + lg],
+                    in1=acc[:, tt, :],
+                    op0=ALU.mult,
+                    op1=ALU.mult,
+                )
+            nc.vector.tensor_tensor(
+                out=av[:, 2 * tp : 2 * tp + 2, :],
+                in0=acc[:],
+                in1=bc[:, 2, j * C : (j + 1) * C].unsqueeze(1).to_broadcast([P, 2, C]),
+                op=ALU.mult,
+            )
+
+        def u_int(j, lg, eng):
+            ug = ub_pool.tile([P, C * PACK], BF16, name="ug", align_bytes=64)
+            interleave(eng, ug, ub_of[j, lg], C)
+            ug_of[j, lg] = ug
+
+        def u_q(j, lg):
+            qu[j, lg] = quantize(ug_of[j, lg], uc_pool, "qu")
+
+        def h_mm(j, g, tp):
+            hp = h_psum.tile([P, 2, C], F32, name="hp")
+            for tt in range(2):
+                for kp in range(2):
+                    mx(hp[:, tt, :], qk[j, g, kp], (2 * tp + tt) * P, qu[j, kp], 0, C, kp == 0, kp == 1)
+            hacc[j, g, tp] = hp
+
+        def h_use(j, g, tp):
+            hp = hacc[j, g, tp]
+            y = sg[g, j // 2][:, :, cols_of(j)]
+            for tt in range(2):
+                t = 2 * tp + tt
+                nc.vector.scalar_tensor_tensor(
+                    out=y[:, t, :],
+                    in0=bc[:, 1, j * C : (j + 1) * C],
+                    scalar=sm[:, t, 2 * j + g : 2 * j + g + 1],
+                    in1=hp[:, tt, :],
+                    op0=ALU.mult,
+                    op1=ALU.add,
+                )
+
+        def y_add(j, g, tp, eng):
+            y = sg[g, j // 2][:, 2 * tp : 2 * tp + 2, cols_of(j)]
+            dv = a[g, j // 2][:, 2 * tp : 2 * tp + 2, cols_of(j)]
+            e = nc.gpsimd if eng == "g" else nc.vector
+            e.tensor_tensor(out=y, in0=y, in1=dv, op=ALU.add)
+
+        def store(j, g, tp):
+            view = out[g * K_PASS : (g + 1) * K_PASS, j * C : (j + 1) * C].rearrange("(m t) c -> m t c", t=PACK)
+            nc.sync.dma_start(
+                out=view[:, 2 * tp : 2 * tp + 2, :], in_=sg[g, j // 2][:, 2 * tp : 2 * tp + 2, cols_of(j)]
+            )
+
+        groups_of = {}
+
+        def k_turn(j, g, half, engs):
+            if (j, g) not in groups_of:
+                groups_of[j, g] = new_groups()
+            turn(rk[j, g, half], half, groups_of[j, g], engs)
+
+        def k_quant(j, g, kp):
+            qk[j, g, kp] = quantize(groups_of[j, g][kp], kc_pool, "qk")
+
+        def x_turn(g, half, engs):
+            if ("x", g) not in groups_of:
+                groups_of["x", g] = new_groups()
+            turn(rx[g, half], half, groups_of["x", g], engs)
+
+        def x_quant(g, kp):
+            qx[g, kp] = quantize(groups_of["x", g][kp], keep, "qx%d%d" % (g, kp))
+
+        wgrp = {}
+
+        def w_int(tag, nh, kp, eng):
+            grp = grp_pool.tile([P, 2048], BF16, name="grp", align_bytes=64)
+            interleave(eng, grp, rw[tag, nh, kp], 512)
+            wgrp[tag, nh, kp] = grp
+
+        def w_quant(tag, nh, kp):
+            qw[tag, nh, kp] = quantize(wgrp[tag, nh, kp], keep, "qw%s%d%d" % (tag, nh, kp))
+
+
+        spread(0,"v")
+        load_one_x(0,1)
+        load_one_w(w_step,"s",0,0)
+        load_one_x(0,0)
+        spread(2,"s")
+        load_x(1)
+        spread(1,"s")
+        w_int("s",0,0,"v")
+        load_one_w(w_step,"s",0,1)
+        x_turn(0,1,"ss")
+        w_quant("s",0,0)
+        x_turn(0,0,"vs")
+        x_turn(1,0,"ss")
+        x_turn(1,1,"ss")
+        x_quant(0,1)
+        x_quant(0,0)
+        load_ws(w_step,"s",1)
+        w_int("s",0,1,"v")
+        x_quant(1,1)
+        prep_cols()
+        w_quant("s",0,1)
+        g_mm(0,0,2)
+        g_mm(0,0,0)
+        g_mm(0,0,3)
+        x_quant(1,0)
+        g_use(0,0,2)
+        load_ws(w_in,"i",0)
+        g_mm(0,0,1)
+        g_use(0,0,0)
+        w_int("s",1,0,"s")
+        g_use(0,0,3)
+        g_mm(1,0,3)
+        w_int("s",1,1,"s")
+        g_use(0,0,1)
+        sig(0,0,0)
+        sig(0,0,1)
+        g_use(1,0,3)
+        g_mm(1,0,2)
+        g_use(1,0,2)
+        w_int("i",0,0,"g")
+        g_mm(1,0,0)
+        load_k(0)
+        w_quant("s",1,0)
+        w_quant("i",0,0)
+        g_mm(1,0,1)
+        w_quant("s",1,1)
+        g_use(1,0,1)
+        g_use(1,0,0)
+        k_turn(0,0,1,"ss")
+        k_turn(0,0,0,"vv")
+        g_mm(0,1,2)
+        g_mm(1,1,0)
+        g_use(0,1,2)
+        g_use(1,1,0)
+        g_mm(0,1,3)
+        g_mm(0,1,0)
+        w_int("i",0,1,"g")
+        g_use(0,1,3)
+        g_use(0,1,0)
+        w_quant("i",0,1)
+        load_ws(w_in,"i",1)
+        sig(1,0,1)
+        g_mm(0,1,1)
+        g_mm(1,1,1)
+        sig(1,0,0)
+        ln(0,0)
+        k_quant(0,0,1)
+        g_mm(1,1,3)
+        ln(1,0)
+        g_use(1,1,3)
+        ln(0,1)
+        g_use(0,1,1)
+        k_quant(0,0,0)
+        k_turn(0,1,0,"vs")
+        m_max(0,0)
+        k_turn(0,1,1,"ss")
+        v_mm(0,0,0)
+        load_k(1)
+        m_max(0,1)
+        ln(1,1)
+        w_int("i",1,0,"s")
+        v_use(0,0,0)
+        g_use(1,1,1)
+        k_turn(1,0,0,"ss")
+        w_int("i",1,1,"g")
+        g_mm(1,1,2)
+        k_quant(0,1,0)
+        k_quant(0,1,1)
+        g_use(1,1,2)
+        v_mm(0,0,1)
+        v_use(0,0,1)
+        v_mm(0,1,0)
+        v_use(0,1,0)
+        u_int(0,0,"s")
+        v_mm(0,1,1)
+        k_turn(1,0,1,"ss")
+        w_quant("i",1,0)
+        v_mm(1,0,1)
+        u_q(0,0)
+        m_max(1,1)
+        k_turn(1,1,0,"ss")
+        m_max(1,0)
+        v_mm(1,1,1)
+        w_quant("i",1,1)
+        v_use(0,1,1)
+        sig(0,1,0)
+        sig(0,1,1)
+        v_use(1,0,1)
+        sig(1,1,1)
+        k_turn(1,1,1,"ss")
+        k_quant(1,0,1)
+        u_int(0,1,"g")
+        sig(1,1,0)
+        k_quant(1,0,0)
+        u_q(0,1)
+        v_mm(1,1,0)
+        h_mm(0,1,1)
+        v_use(1,1,0)
+        v_mm(1,0,0)
+        h_mm(0,1,0)
+        v_use(1,1,1)
+        ln(2,0)
+        k_quant(1,1,1)
+        h_mm(0,0,1)
+        h_use(0,1,1)
+        ln(2,1)
+        ln(3,1)
+        v_use(1,0,0)
+        h_use(0,1,0)
+        load_k(3)
+        y_add(0,1,1,"g")
+        v_mm(2,0,1)
+        m_max(2,0)
+        v_mm(2,0,0)
+        k_quant(1,1,0)
+        load_k(2)
+        k_turn(2,0,1,"ss")
+        h_use(0,0,1)
+        v_use(2,0,1)
+        h_mm(0,0,0)
+        k_turn(2,0,0,"ss")
+        u_int(1,0,"s")
+        v_use(2,0,0)
+        v_mm(2,1,1)
+        k_turn(3,1,0,"ss")
+        k_turn(3,1,1,"ss")
+        v_mm(3,0,1)
+        ln(3,0)
+        y_add(0,1,0,"g")
+        u_int(1,1,"g")
+        u_int(2,0,"s")
+        h_use(0,0,0)
+        m_max(2,1)
+        v_mm(2,1,0)
+        y_add(0,0,0,"g")
+        u_q(1,1)
+        k_turn(2,1,0,"ss")
+        y_add(0,0,1,"g")
+        store(0,0,0)
+        u_q(1,0)
+        k_quant(2,0,0)
+        h_mm(1,0,0)
+        k_quant(3,1,0)
+        h_mm(1,0,1)
+        k_quant(2,0,1)
+        m_max(3,1)
+        k_turn(3,0,0,"ss")
+        v_use(2,1,1)
+        h_use(1,0,0)
+        h_use(1,0,1)
+        h_mm(1,1,1)
+        store(0,1,1)
+        k_turn(2,1,1,"ss")
+        h_mm(1,1,0)
+        y_add(1,0,0,"g")
+        u_q(2,0)
+        m_max(3,0)
+        h_use(1,1,1)
+        v_mm(3,1,1)
+        v_use(3,0,1)
+        y_add(1,0,1,"g")
+        v_use(2,1,0)
+        k_quant(2,1,1)
+        v_mm(3,1,0)
+        store(1,0,0)
+        u_int(2,1,"s")
+        k_quant(2,1,0)
+        u_q(2,1)
+        h_mm(2,1,1)
+        h_mm(2,0,1)
+        h_use(1,1,0)
+        store(1,0,1)
+        k_quant(3,1,1)
+        h_use(2,1,1)
+        y_add(1,1,0,"g")
+        y_add(1,1,1,"g")
+        v_mm(3,0,0)
+        h_use(2,0,1)
+        v_use(3,0,0)
+        u_int(3,0,"s")
+        store(0,1,0)
+        y_add(2,0,1,"g")
+        v_use(3,1,1)
+        v_use(3,1,0)
+        k_turn(3,0,1,"ss")
+        k_quant(3,0,0)
+        u_q(3,0)
+        u_int(3,1,"s")
+        k_quant(3,0,1)
+        h_mm(2,0,0)
+        u_q(3,1)
+        h_mm(3,0,0)
+        y_add(2,1,1,"g")
+        h_use(2,0,0)
+        h_mm(3,0,1)
+        y_add(2,0,0,"g")
+        h_use(3,0,0)
+        h_mm(3,1,0)
+        h_use(3,0,1)
+        store(2,1,1)
+        h_mm(3,1,1)
+        h_use(3,1,0)
+        h_mm(2,1,0)
+        y_add(3,0,1,"v")
+        h_use(3,1,1)
+        y_add(3,0,0,"g")
+        store(2,0,1)
+        store(1,1,1)
+        h_use(2,1,0)
+        y_add(3,1,1,"v")
+        y_add(3,1,0,"g")
+        store(1,1,0)
+        store(0,0,1)
+        store(3,0,0)
+        store(3,0,1)
+        store(2,0,0)
+        store(3,1,0)
+        store(3,1,1)
+        y_add(2,1,0,"v")
+        store(2,1,0)

@@ -40,20 +40,21 @@ def tile_step_weighted_time_kernel_f4_kernel(
 
         dummy = keep.tile([P, 1], F32, name="dummy")
         nc.vector.memset(dummy[:], 0.0)
-        nc.scalar.activation(out=dummy[:], in_=dummy[:], func=ACT.Sigmoid)
         rows = keep.tile([P, K_PASS], BF16, name="rows")
         vecs = keep.tile([P, N], BF16, name="vecs")
         nc.vector.memset(rows[:], 0.0)
         nc.vector.memset(vecs[:], 0.0)
         ident = keep.tile([P, P], F32, name="ident")
         make_identity(nc, ident[:])
-        ident_b = keep.tile([P, P], BF16, name="ident_b")
-        nc.vector.tensor_copy(out=ident_b[:], in_=ident[:])
         nc.scalar.dma_start(out=vecs[0:1, :], in_=b_step.unsqueeze(0))
         nc.scalar.dma_start(out=vecs[1:2, :], in_=h0.unsqueeze(0))
         nc.scalar.dma_start(out=vecs[2:3, :], in_=d.unsqueeze(0))
         nc.scalar.dma_start(out=rows[0:8, :], in_=alpha.rearrange("h (g q) -> (h g) q", q=K_PASS))
         nc.scalar.dma_start(out=rows[8:10, :], in_=tau.rearrange("(g q) -> g q", q=K_PASS))
+        nc.scalar.activation(out=dummy[:], in_=dummy[:], func=ACT.Sigmoid)
+
+        ident_b = keep.tile([P, P], BF16, name="ident_b")
+        nc.vector.tensor_copy(out=ident_b[:], in_=ident[:])
 
         def load_rows(src, g, half):
             raw = raw_pool.tile([P, 2, 1024], BF16, name="raw", align_bytes=64)
@@ -337,243 +338,243 @@ def tile_step_weighted_time_kernel_f4_kernel(
             qw[tag, nh, kp] = quantize(wgrp[tag, nh, kp], keep, "qw%s%d%d" % (tag, nh, kp))
 
 
-        spread(0,"v")
-        load_one_x(0,1)
-        load_one_w(w_step,"s",0,0)
-        load_one_x(0,0)
-        spread(2,"s")
         load_x(1)
-        spread(1,"s")
-        w_int("s",0,0,"v")
+        load_one_w(w_step,"s",0,0)
         load_one_w(w_step,"s",0,1)
-        x_turn(0,1,"ss")
-        w_quant("s",0,0)
-        x_turn(0,0,"vs")
-        x_turn(1,0,"ss")
+        x_turn(1,0,"sv")
+        w_int("s",0,0,"s")
         x_turn(1,1,"ss")
-        x_quant(0,1)
-        x_quant(0,0)
-        load_ws(w_step,"s",1)
         w_int("s",0,1,"v")
-        x_quant(1,1)
-        prep_cols()
-        w_quant("s",0,1)
-        g_mm(0,0,2)
-        g_mm(0,0,0)
-        g_mm(0,0,3)
-        x_quant(1,0)
-        g_use(0,0,2)
-        load_ws(w_in,"i",0)
-        g_mm(0,0,1)
-        g_use(0,0,0)
+        load_ws(w_step,"s",1)
         w_int("s",1,0,"s")
-        g_use(0,0,3)
-        g_mm(1,0,3)
-        w_int("s",1,1,"s")
-        g_use(0,0,1)
-        sig(0,0,0)
-        sig(0,0,1)
-        g_use(1,0,3)
-        g_mm(1,0,2)
-        g_use(1,0,2)
-        w_int("i",0,0,"g")
+        w_quant("s",0,1)
+        w_quant("s",0,0)
+        x_quant(1,1)
+        load_one_x(0,1)
+        load_one_x(0,0)
+        x_quant(1,0)
+        prep_cols()
+        spread(0,"v")
+        spread(1,"v")
+        x_turn(0,1,"ss")
         g_mm(1,0,0)
-        load_k(0)
-        w_quant("s",1,0)
-        w_quant("i",0,0)
-        g_mm(1,0,1)
-        w_quant("s",1,1)
-        g_use(1,0,1)
+        x_turn(0,0,"ss")
         g_use(1,0,0)
-        k_turn(0,0,1,"ss")
-        k_turn(0,0,0,"vv")
-        g_mm(0,1,2)
-        g_mm(1,1,0)
-        g_use(0,1,2)
-        g_use(1,1,0)
-        g_mm(0,1,3)
-        g_mm(0,1,0)
+        w_int("s",1,1,"g")
+        w_quant("s",1,0)
+        g_mm(1,0,1)
+        x_quant(0,0)
+        load_ws(w_in,"i",0)
+        x_quant(0,1)
+        load_k(1)
+        g_mm(1,0,2)
+        w_quant("s",1,1)
+        w_int("i",0,0,"s")
+        g_use(1,0,1)
+        k_turn(1,0,0,"ss")
         w_int("i",0,1,"g")
+        g_use(1,0,2)
+        g_mm(0,0,3)
+        g_use(0,0,3)
+        g_mm(0,0,1)
+        load_ws(w_in,"i",1)
+        g_mm(0,0,2)
+        g_use(0,0,1)
+        g_mm(0,0,0)
+        sig(1,0,0)
+        g_use(0,0,2)
+        g_mm(1,1,2)
+        g_use(0,0,0)
+        g_mm(0,1,3)
+        g_use(1,1,2)
         g_use(0,1,3)
+        g_mm(1,0,3)
+        g_mm(1,1,3)
+        g_mm(0,1,0)
+        g_use(1,0,3)
+        w_int("i",1,0,"g")
+        sig(0,0,1)
+        g_use(1,1,3)
+        sig(0,0,0)
         g_use(0,1,0)
         w_quant("i",0,1)
-        load_ws(w_in,"i",1)
-        sig(1,0,1)
-        g_mm(0,1,1)
         g_mm(1,1,1)
-        sig(1,0,0)
-        ln(0,0)
-        k_quant(0,0,1)
-        g_mm(1,1,3)
-        ln(1,0)
-        g_use(1,1,3)
-        ln(0,1)
-        g_use(0,1,1)
-        k_quant(0,0,0)
-        k_turn(0,1,0,"vs")
-        m_max(0,0)
-        k_turn(0,1,1,"ss")
-        v_mm(0,0,0)
-        load_k(1)
-        m_max(0,1)
-        ln(1,1)
-        w_int("i",1,0,"s")
-        v_use(0,0,0)
-        g_use(1,1,1)
-        k_turn(1,0,0,"ss")
-        w_int("i",1,1,"g")
-        g_mm(1,1,2)
-        k_quant(0,1,0)
-        k_quant(0,1,1)
-        g_use(1,1,2)
-        v_mm(0,0,1)
-        v_use(0,0,1)
-        v_mm(0,1,0)
-        v_use(0,1,0)
-        u_int(0,0,"s")
-        v_mm(0,1,1)
+        sig(1,0,1)
         k_turn(1,0,1,"ss")
+        ln(0,0)
+        g_mm(0,1,1)
+        w_quant("i",0,0)
+        g_mm(0,1,2)
         w_quant("i",1,0)
-        v_mm(1,0,1)
-        u_q(0,0)
-        m_max(1,1)
-        k_turn(1,1,0,"ss")
-        m_max(1,0)
+        g_mm(1,1,0)
+        k_quant(1,0,0)
+        ln(1,1)
+        g_use(1,1,1)
+        ln(0,1)
+        g_use(0,1,2)
+        load_k(0)
+        g_use(0,1,1)
+        g_use(1,1,0)
+        ln(1,0)
+        k_quant(1,0,1)
+        spread(2,"s")
         v_mm(1,1,1)
-        w_quant("i",1,1)
-        v_use(0,1,1)
+        m_max(0,0)
+        k_turn(0,1,0,"ss")
         sig(0,1,0)
+        m_max(1,1)
+        w_int("i",1,1,"g")
+        m_max(0,1)
+        v_mm(1,1,0)
+        v_mm(1,0,1)
+        m_max(1,0)
+        k_turn(1,1,1,"ss")
+        v_use(1,1,1)
+        v_mm(1,0,0)
+        v_use(1,1,0)
+        v_mm(0,0,1)
+        v_mm(0,0,0)
         sig(0,1,1)
         v_use(1,0,1)
-        sig(1,1,1)
-        k_turn(1,1,1,"ss")
-        k_quant(1,0,1)
-        u_int(0,1,"g")
-        sig(1,1,0)
-        k_quant(1,0,0)
-        u_q(0,1)
-        v_mm(1,1,0)
-        h_mm(0,1,1)
-        v_use(1,1,0)
-        v_mm(1,0,0)
-        h_mm(0,1,0)
-        v_use(1,1,1)
-        ln(2,0)
-        k_quant(1,1,1)
-        h_mm(0,0,1)
-        h_use(0,1,1)
-        ln(2,1)
-        ln(3,1)
         v_use(1,0,0)
-        h_use(0,1,0)
-        load_k(3)
-        y_add(0,1,1,"g")
-        v_mm(2,0,1)
-        m_max(2,0)
-        v_mm(2,0,0)
-        k_quant(1,1,0)
-        load_k(2)
-        k_turn(2,0,1,"ss")
-        h_use(0,0,1)
-        v_use(2,0,1)
-        h_mm(0,0,0)
-        k_turn(2,0,0,"ss")
-        u_int(1,0,"s")
-        v_use(2,0,0)
-        v_mm(2,1,1)
-        k_turn(3,1,0,"ss")
-        k_turn(3,1,1,"ss")
-        v_mm(3,0,1)
-        ln(3,0)
-        y_add(0,1,0,"g")
+        k_turn(1,1,0,"ss")
+        v_use(0,0,1)
         u_int(1,1,"g")
-        u_int(2,0,"s")
-        h_use(0,0,0)
-        m_max(2,1)
-        v_mm(2,1,0)
-        y_add(0,0,0,"g")
-        u_q(1,1)
-        k_turn(2,1,0,"ss")
-        y_add(0,0,1,"g")
-        store(0,0,0)
+        v_use(0,0,0)
+        k_quant(1,1,0)
+        u_int(1,0,"g")
+        sig(1,1,1)
+        v_mm(0,1,1)
+        load_k(2)
+        load_k(3)
         u_q(1,0)
-        k_quant(2,0,0)
-        h_mm(1,0,0)
-        k_quant(3,1,0)
+        k_turn(0,1,1,"ss")
+        u_q(1,1)
+        w_quant("i",1,1)
+        v_mm(0,1,0)
+        v_use(0,1,1)
         h_mm(1,0,1)
-        k_quant(2,0,1)
-        m_max(3,1)
-        k_turn(3,0,0,"ss")
-        v_use(2,1,1)
-        h_use(1,0,0)
+        sig(1,1,0)
+        v_use(0,1,0)
+        ln(2,1)
+        u_int(0,1,"s")
+        v_mm(2,1,0)
         h_use(1,0,1)
-        h_mm(1,1,1)
-        store(0,1,1)
-        k_turn(2,1,1,"ss")
+        v_mm(2,0,1)
+        k_quant(0,1,0)
+        k_quant(1,1,1)
+        ln(2,0)
+        u_int(0,0,"g")
+        v_mm(2,1,1)
+        k_quant(0,1,1)
         h_mm(1,1,0)
-        y_add(1,0,0,"g")
-        u_q(2,0)
-        m_max(3,0)
-        h_use(1,1,1)
-        v_mm(3,1,1)
-        v_use(3,0,1)
-        y_add(1,0,1,"g")
+        m_max(2,1)
+        u_q(0,0)
+        k_turn(0,0,0,"ss")
         v_use(2,1,0)
-        k_quant(2,1,1)
-        v_mm(3,1,0)
-        store(1,0,0)
-        u_int(2,1,"s")
-        k_quant(2,1,0)
-        u_q(2,1)
-        h_mm(2,1,1)
-        h_mm(2,0,1)
         h_use(1,1,0)
-        store(1,0,1)
-        k_quant(3,1,1)
-        h_use(2,1,1)
+        h_mm(1,0,0)
+        k_turn(2,1,0,"ss")
+        ln(3,1)
+        u_q(0,1)
+        h_use(1,0,0)
+        v_mm(2,0,0)
+        h_mm(0,1,0)
+        m_max(2,0)
+        k_turn(2,1,1,"ss")
+        k_turn(0,0,1,"ss")
+        h_use(0,1,0)
+        v_use(2,1,1)
+        v_use(2,0,1)
+        h_mm(1,1,1)
+        u_int(2,1,"s")
+        y_add(1,0,1,"g")
+        v_mm(3,0,1)
+        v_use(2,0,0)
+        ln(3,0)
+        k_turn(2,0,1,"ss")
+        k_turn(2,0,0,"ss")
+        k_quant(0,0,0)
+        k_quant(0,0,1)
+        m_max(3,1)
+        m_max(3,0)
+        k_quant(2,1,1)
+        h_use(1,1,1)
+        y_add(1,0,0,"g")
+        k_quant(2,0,1)
+        v_mm(3,1,0)
+        h_mm(0,0,0)
+        u_q(2,1)
         y_add(1,1,0,"g")
-        y_add(1,1,1,"g")
-        v_mm(3,0,0)
-        h_use(2,0,1)
-        v_use(3,0,0)
-        u_int(3,0,"s")
-        store(0,1,0)
-        y_add(2,0,1,"g")
-        v_use(3,1,1)
+        k_quant(2,0,0)
+        y_add(0,1,0,"g")
+        u_int(2,0,"s")
         v_use(3,1,0)
+        h_use(0,0,0)
+        v_mm(3,1,1)
+        u_q(2,0)
+        k_turn(3,1,1,"ss")
+        k_turn(3,0,0,"ss")
+        h_mm(0,0,1)
+        k_quant(2,1,0)
+        h_mm(2,1,1)
+        y_add(1,1,1,"g")
         k_turn(3,0,1,"ss")
-        k_quant(3,0,0)
-        u_q(3,0)
-        u_int(3,1,"s")
-        k_quant(3,0,1)
+        h_use(0,0,1)
+        h_mm(0,1,1)
         h_mm(2,0,0)
-        u_q(3,1)
-        h_mm(3,0,0)
-        y_add(2,1,1,"g")
-        h_use(2,0,0)
-        h_mm(3,0,1)
-        y_add(2,0,0,"g")
-        h_use(3,0,0)
-        h_mm(3,1,0)
-        h_use(3,0,1)
-        store(2,1,1)
-        h_mm(3,1,1)
-        h_use(3,1,0)
-        h_mm(2,1,0)
-        y_add(3,0,1,"v")
-        h_use(3,1,1)
-        y_add(3,0,0,"g")
-        store(2,0,1)
         store(1,1,1)
-        h_use(2,1,0)
-        y_add(3,1,1,"v")
-        y_add(3,1,0,"g")
+        y_add(0,0,0,"g")
+        v_mm(3,0,0)
+        v_use(3,1,1)
+        store(0,0,0)
+        h_use(2,1,1)
+        y_add(0,0,1,"g")
+        v_use(3,0,1)
+        y_add(2,1,1,"g")
+        h_use(0,1,1)
+        k_quant(3,0,1)
         store(1,1,0)
-        store(0,0,1)
-        store(3,0,0)
-        store(3,0,1)
-        store(2,0,0)
-        store(3,1,0)
-        store(3,1,1)
+        v_use(3,0,0)
+        store(2,1,1)
+        u_int(3,1,"s")
+        store(1,0,0)
+        y_add(0,1,1,"g")
+        store(0,1,0)
+        u_int(3,0,"s")
+        h_use(2,0,0)
+        k_quant(3,0,0)
+        k_turn(3,1,0,"ss")
+        u_q(3,1)
+        u_q(3,0)
+        h_mm(2,1,0)
+        h_mm(3,0,1)
+        k_quant(3,1,0)
+        store(0,1,1)
+        k_quant(3,1,1)
+        h_mm(3,0,0)
+        h_mm(3,1,1)
+        store(1,0,1)
+        h_use(2,1,0)
+        y_add(2,0,0,"g")
+        h_use(3,0,1)
         y_add(2,1,0,"v")
+        h_use(3,0,0)
+        h_mm(2,0,1)
+        store(2,0,0)
+        y_add(3,0,1,"g")
+        h_use(3,1,1)
+        y_add(3,0,0,"v")
         store(2,1,0)
+        h_mm(3,1,0)
+        h_use(2,0,1)
+        h_use(3,1,0)
+        store(0,0,1)
+        y_add(2,0,1,"v")
+        y_add(3,1,1,"g")
+        store(3,0,1)
+        store(3,0,0)
+        store(3,1,1)
+        y_add(3,1,0,"v")
+        store(2,0,1)
+        store(3,1,0)

@@ -62,6 +62,12 @@ def tile_step_weighted_time_kernel_f4_kernel(
             nc.sync.dma_start(out=raw[:], in_=view[:, 2 * half : 2 * half + 2, :])
             return raw
 
+        def load_w_part(w, kp, c0):
+            raw = raw_pool.tile([P, PACK, 256], BF16, name="raw", align_bytes=64)
+            view = w[kp * K_PASS : (kp + 1) * K_PASS, c0 : c0 + 256]
+            nc.sync.dma_start(out=raw[:], in_=view.rearrange("(p j) n -> p j n", j=PACK))
+            return raw
+
         def load_w(w, nh, kp):
             raw = raw_pool.tile([P, PACK, 512], BF16, name="raw", align_bytes=64)
             view = w[kp * K_PASS : (kp + 1) * K_PASS, nh * 512 : (nh + 1) * 512]
@@ -109,16 +115,32 @@ def tile_step_weighted_time_kernel_f4_kernel(
             nc.vector.quantize_mx(out=codes[:].bitcast(FP8X4), scales=scales[:], in_=grp[:])
             return codes, scales
 
-        def interleave(eng, grp, raw, width):
-            copy(
-                eng,
-                grp[:].rearrange("p (c i t) -> p c t i", i=4, t=PACK),
-                raw[:].rearrange("p t (c i) -> p c t i", i=4),
+        def interleave(eng, dst, raw):
+            if eng == "g":
+                copy(eng, dst.rearrange("p (c t) -> p c t", t=PACK), raw[:].rearrange("p t c -> p c t"))
+            else:
+                copy(
+                    eng,
+                    dst.rearrange("p (c i t) -> p c t i", i=4, t=PACK),
+                    raw[:].rearrange("p t (c i) -> p c t i", i=4),
+                )
+
+        def quantize_half(grp, half, planes):
+            cols = slice(256 * half, 256 * (half + 1))
+            nc.vector.quantize_mx(
+                out=planes[0][:, cols].bitcast(FP8X4),
+                scales=planes[1][:, cols],
+                in_=grp[:, 1024 * half : 1024 * (half + 1)],
             )
+
+        def new_planes(pool, name):
+            codes = pool.tile([P, 512], U32, name=name + "_c", align_bytes=64)
+            scales = pool.tile([P, 512], U8, name=name + "_s", align_bytes=64)
+            return codes, scales
 
         def prep_w(raw, eng, name):
             grp = grp_pool.tile([P, 2048], BF16, name="grp", align_bytes=64)
-            interleave(eng, grp, raw, 512)
+            interleave(eng, grp[:], raw)
             return quantize(grp, keep, name)
 
         def mx(out_ap, stat, c0, mov, n0, width, start, stop):
@@ -143,6 +165,9 @@ def tile_step_weighted_time_kernel_f4_kernel(
         def load_ws(w, tag, nh):
             for kp in range(2):
                 rw[tag, nh, kp] = load_w(w, nh, kp)
+
+        def load_one_k(j, g, half):
+            rk[j, g, half] = load_rows(kernel[j], g, half)
 
         def load_one_x(g, half):
             rx[g, half] = load_rows(x, g, half)
@@ -270,7 +295,7 @@ def tile_step_weighted_time_kernel_f4_kernel(
 
         def u_int(j, lg, eng):
             ug = ub_pool.tile([P, C * PACK], BF16, name="ug", align_bytes=64)
-            interleave(eng, ug, ub_of[j, lg], C)
+            interleave(eng, ug[:], ub_of[j, lg])
             ug_of[j, lg] = ug
 
         def u_q(j, lg):
@@ -324,257 +349,301 @@ def tile_step_weighted_time_kernel_f4_kernel(
                 groups_of["x", g] = new_groups()
             turn(rx[g, half], half, groups_of["x", g], engs)
 
-        def x_quant(g, kp):
-            qx[g, kp] = quantize(groups_of["x", g][kp], keep, "qx%d%d" % (g, kp))
+        for g in range(2):
+            for kp in range(2):
+                qx[g, kp] = new_planes(keep, "qx%d%d" % (g, kp))
+                if g == 0:
+                    qw["s", 0, kp] = new_planes(keep, "qws0%d" % kp)
 
         wgrp = {}
 
+        def x_quant(g, kp, half):
+            quantize_half(groups_of["x", g][kp], half, qx[g, kp])
+
+        def load_first(kp, half):
+            rw["s", 0, kp, half] = load_w_part(w_step, kp, 256 * half)
+
+        def first_int(kp, half, eng):
+            if ("s", 0, kp) not in wgrp:
+                grp = grp_pool.tile([P, 2048], BF16, name="grp", align_bytes=64)
+                wgrp["s", 0, kp] = grp
+            interleave(eng, wgrp["s", 0, kp][:, 1024 * half : 1024 * (half + 1)], rw["s", 0, kp, half])
+
+        def first_quant(kp, half):
+            quantize_half(wgrp["s", 0, kp], half, qw["s", 0, kp])
+
         def w_int(tag, nh, kp, eng):
             grp = grp_pool.tile([P, 2048], BF16, name="grp", align_bytes=64)
-            interleave(eng, grp, rw[tag, nh, kp], 512)
+            interleave(eng, grp[:], rw[tag, nh, kp])
             wgrp[tag, nh, kp] = grp
 
         def w_quant(tag, nh, kp):
             qw[tag, nh, kp] = quantize(wgrp[tag, nh, kp], keep, "qw%s%d%d" % (tag, nh, kp))
 
 
-        load_x(1)
-        load_one_w(w_step,"s",0,0)
-        load_one_w(w_step,"s",0,1)
-        x_turn(1,0,"sv")
-        w_int("s",0,0,"s")
-        x_turn(1,1,"ss")
-        w_int("s",0,1,"v")
-        load_ws(w_step,"s",1)
-        w_int("s",1,0,"s")
-        w_quant("s",0,1)
-        w_quant("s",0,0)
-        x_quant(1,1)
+        load_first(1,0)
+        load_one_x(1,1)
+        load_one_x(1,0)
+        x_turn(1,1,"vv")
+        load_first(1,1)
+        load_first(0,0)
+        first_int(0,0,"s")
+        first_int(1,0,"g")
+        load_first(0,1)
+        first_int(1,1,"g")
+        first_quant(1,0)
+        spread(2,"v")
+        first_quant(1,1)
+        x_quant(1,1,1)
         load_one_x(0,1)
+        first_int(0,1,"v")
+        first_quant(0,0)
+        x_turn(1,0,"ss")
         load_one_x(0,0)
-        x_quant(1,0)
-        prep_cols()
-        spread(0,"v")
-        spread(1,"v")
+        x_quant(1,0,1)
+        load_one_w(w_step,"s",1,1)
+        load_one_w(w_step,"s",1,0)
+        spread(0,"s")
         x_turn(0,1,"ss")
-        g_mm(1,0,0)
         x_turn(0,0,"ss")
-        g_use(1,0,0)
-        w_int("s",1,1,"g")
-        w_quant("s",1,0)
+        w_int("s",1,0,"s")
+        load_one_w(w_in,"i",1,1)
+        x_quant(1,0,0)
+        x_quant(1,1,0)
+        load_one_w(w_in,"i",0,1)
+        first_quant(0,1)
         g_mm(1,0,1)
-        x_quant(0,0)
-        load_ws(w_in,"i",0)
-        x_quant(0,1)
-        load_k(1)
+        x_quant(0,0,1)
+        w_int("s",1,1,"v")
+        w_int("i",0,1,"s")
+        x_quant(0,0,0)
+        x_quant(0,1,1)
+        g_mm(0,0,2)
         g_mm(1,0,2)
         w_quant("s",1,1)
-        w_int("i",0,0,"s")
-        g_use(1,0,1)
-        k_turn(1,0,0,"ss")
-        w_int("i",0,1,"g")
-        g_use(1,0,2)
+        load_one_w(w_in,"i",0,0)
         g_mm(0,0,3)
+        g_use(1,0,1)
+        load_one_k(0,0,1)
+        g_use(0,0,2)
+        g_use(1,0,2)
+        g_mm(1,0,0)
+        load_one_k(1,0,0)
         g_use(0,0,3)
+        sig(0,0,1)
+        load_one_k(1,1,1)
+        g_use(1,0,0)
+        prep_cols()
+        x_quant(0,1,0)
+        w_quant("s",1,0)
+        g_mm(1,0,3)
+        load_one_w(w_in,"i",1,0)
         g_mm(0,0,1)
-        load_ws(w_in,"i",1)
-        g_mm(0,0,2)
+        g_use(1,0,3)
+        g_mm(0,1,3)
         g_use(0,0,1)
         g_mm(0,0,0)
-        sig(1,0,0)
-        g_use(0,0,2)
-        g_mm(1,1,2)
-        g_use(0,0,0)
-        g_mm(0,1,3)
-        g_use(1,1,2)
-        g_use(0,1,3)
-        g_mm(1,0,3)
-        g_mm(1,1,3)
-        g_mm(0,1,0)
-        g_use(1,0,3)
-        w_int("i",1,0,"g")
-        sig(0,0,1)
-        g_use(1,1,3)
-        sig(0,0,0)
-        g_use(0,1,0)
-        w_quant("i",0,1)
-        g_mm(1,1,1)
-        sig(1,0,1)
-        k_turn(1,0,1,"ss")
-        ln(0,0)
-        g_mm(0,1,1)
-        w_quant("i",0,0)
-        g_mm(0,1,2)
-        w_quant("i",1,0)
-        g_mm(1,1,0)
-        k_quant(1,0,0)
-        ln(1,1)
-        g_use(1,1,1)
-        ln(0,1)
-        g_use(0,1,2)
-        load_k(0)
-        g_use(0,1,1)
-        g_use(1,1,0)
-        ln(1,0)
-        k_quant(1,0,1)
-        spread(2,"s")
-        v_mm(1,1,1)
-        m_max(0,0)
-        k_turn(0,1,0,"ss")
-        sig(0,1,0)
-        m_max(1,1)
         w_int("i",1,1,"g")
-        m_max(0,1)
+        load_one_k(0,1,0)
+        g_use(0,1,3)
+        g_use(0,0,0)
+        g_mm(0,1,1)
+        sig(1,0,0)
+        sig(1,0,1)
+        sig(0,0,0)
+        ln(1,1)
+        g_mm(0,1,0)
+        w_int("i",0,0,"g")
+        g_use(0,1,1)
+        g_mm(0,1,2)
+        w_quant("i",1,1)
+        ln(1,0)
+        ln(0,0)
+        load_one_k(1,0,1)
+        w_quant("i",0,0)
+        g_use(0,1,0)
+        w_int("i",1,0,"g")
+        g_mm(1,1,3)
+        g_use(0,1,2)
+        load_one_k(2,1,1)
+        g_mm(1,1,1)
+        g_use(1,1,3)
+        g_use(1,1,1)
+        load_one_k(2,0,1)
+        g_mm(1,1,0)
+        load_one_k(1,1,0)
+        load_one_k(0,0,0)
+        g_use(1,1,0)
+        k_turn(1,0,0,"ss")
+        w_quant("i",0,1)
+        w_quant("i",1,0)
+        load_one_k(0,1,1)
         v_mm(1,1,0)
-        v_mm(1,0,1)
-        m_max(1,0)
-        k_turn(1,1,1,"ss")
-        v_use(1,1,1)
+        v_mm(1,1,1)
+        m_max(1,1)
         v_mm(1,0,0)
+        m_max(1,0)
+        load_one_k(3,1,1)
+        ln(0,1)
         v_use(1,1,0)
+        k_turn(1,0,1,"ss")
+        sig(1,1,0)
         v_mm(0,0,1)
-        v_mm(0,0,0)
-        sig(0,1,1)
-        v_use(1,0,1)
+        load_one_k(2,0,0)
+        m_max(0,0)
+        v_use(1,1,1)
+        v_mm(1,0,1)
+        g_mm(1,1,2)
+        k_turn(1,1,1,"ss")
         v_use(1,0,0)
-        k_turn(1,1,0,"ss")
-        v_use(0,0,1)
         u_int(1,1,"g")
-        v_use(0,0,0)
-        k_quant(1,1,0)
+        v_use(1,0,1)
+        g_use(1,1,2)
+        v_use(0,0,1)
+        k_turn(1,1,0,"ss")
         u_int(1,0,"g")
+        m_max(0,1)
+        u_q(1,1)
+        sig(0,1,0)
+        v_mm(0,0,0)
+        u_q(1,0)
         sig(1,1,1)
         v_mm(0,1,1)
-        load_k(2)
-        load_k(3)
-        u_q(1,0)
-        k_turn(0,1,1,"ss")
-        u_q(1,1)
-        w_quant("i",1,1)
-        v_mm(0,1,0)
-        v_use(0,1,1)
+        k_quant(1,0,0)
+        spread(1,"s")
+        k_quant(1,0,1)
+        v_use(0,0,0)
+        sig(0,1,1)
         h_mm(1,0,1)
-        sig(1,1,0)
-        v_use(0,1,0)
         ln(2,1)
-        u_int(0,1,"s")
-        v_mm(2,1,0)
+        v_use(0,1,1)
         h_use(1,0,1)
-        v_mm(2,0,1)
-        k_quant(0,1,0)
+        k_quant(1,1,0)
+        k_turn(0,0,0,"ss")
+        h_mm(1,0,0)
+        v_mm(0,1,0)
         k_quant(1,1,1)
-        ln(2,0)
-        u_int(0,0,"g")
+        h_mm(1,1,1)
         v_mm(2,1,1)
-        k_quant(0,1,1)
+        k_turn(0,0,1,"ss")
+        v_use(0,1,0)
+        h_use(1,0,0)
+        u_int(0,1,"s")
+        u_int(0,0,"g")
+        v_mm(2,1,0)
+        k_turn(0,1,0,"ss")
+        ln(2,0)
+        y_add(1,0,1,"g")
         h_mm(1,1,0)
         m_max(2,1)
-        u_q(0,0)
-        k_turn(0,0,0,"ss")
-        v_use(2,1,0)
-        h_use(1,1,0)
-        h_mm(1,0,0)
-        k_turn(2,1,0,"ss")
-        ln(3,1)
-        u_q(0,1)
-        h_use(1,0,0)
-        v_mm(2,0,0)
-        h_mm(0,1,0)
-        m_max(2,0)
-        k_turn(2,1,1,"ss")
-        k_turn(0,0,1,"ss")
-        h_use(0,1,0)
+        k_turn(0,1,1,"ss")
+        h_use(1,1,1)
         v_use(2,1,1)
-        v_use(2,0,1)
-        h_mm(1,1,1)
+        v_use(2,1,0)
+        y_add(1,0,0,"g")
+        u_q(0,1)
+        k_quant(0,0,1)
         u_int(2,1,"s")
-        y_add(1,0,1,"g")
+        load_one_k(3,0,0)
+        h_use(1,1,0)
+        u_q(0,0)
+        v_mm(2,0,0)
+        k_quant(0,0,0)
+        k_quant(0,1,0)
+        k_turn(2,0,1,"ss")
+        ln(3,0)
+        ln(3,1)
+        y_add(1,1,1,"g")
+        h_mm(0,0,1)
+        v_mm(2,0,1)
+        m_max(2,0)
+        load_one_k(3,1,0)
+        h_use(0,0,1)
+        k_quant(0,1,1)
         v_mm(3,0,1)
         v_use(2,0,0)
-        ln(3,0)
-        k_turn(2,0,1,"ss")
-        k_turn(2,0,0,"ss")
-        k_quant(0,0,0)
-        k_quant(0,0,1)
-        m_max(3,1)
-        m_max(3,0)
-        k_quant(2,1,1)
-        h_use(1,1,1)
-        y_add(1,0,0,"g")
-        k_quant(2,0,1)
-        v_mm(3,1,0)
-        h_mm(0,0,0)
-        u_q(2,1)
-        y_add(1,1,0,"g")
-        k_quant(2,0,0)
-        y_add(0,1,0,"g")
-        u_int(2,0,"s")
-        v_use(3,1,0)
-        h_use(0,0,0)
-        v_mm(3,1,1)
-        u_q(2,0)
-        k_turn(3,1,1,"ss")
-        k_turn(3,0,0,"ss")
-        h_mm(0,0,1)
-        k_quant(2,1,0)
-        h_mm(2,1,1)
-        y_add(1,1,1,"g")
-        k_turn(3,0,1,"ss")
-        h_use(0,0,1)
-        h_mm(0,1,1)
-        h_mm(2,0,0)
-        store(1,1,1)
-        y_add(0,0,0,"g")
-        v_mm(3,0,0)
-        v_use(3,1,1)
-        store(0,0,0)
-        h_use(2,1,1)
+        v_use(2,0,1)
         y_add(0,0,1,"g")
+        k_turn(2,1,1,"ss")
+        h_mm(0,1,0)
+        y_add(1,1,0,"g")
+        h_mm(0,0,0)
+        h_use(0,1,0)
+        v_mm(3,1,0)
+        u_int(2,0,"s")
+        load_one_k(2,1,0)
+        u_q(2,1)
+        m_max(3,0)
+        h_mm(0,1,1)
+        k_turn(2,0,0,"ss")
+        m_max(3,1)
         v_use(3,0,1)
-        y_add(2,1,1,"g")
+        v_mm(3,1,1)
+        k_turn(2,1,0,"ss")
+        h_use(0,0,0)
+        u_q(2,0)
+        v_mm(3,0,0)
+        store(0,0,1)
+        k_quant(2,1,0)
+        k_turn(3,0,0,"ss")
+        k_quant(2,1,1)
+        y_add(0,1,0,"g")
+        h_mm(2,1,1)
+        k_turn(3,1,1,"ss")
+        y_add(0,0,0,"g")
+        k_quant(2,0,0)
+        k_quant(2,0,1)
         h_use(0,1,1)
-        k_quant(3,0,1)
-        store(1,1,0)
-        v_use(3,0,0)
-        store(2,1,1)
-        u_int(3,1,"s")
-        store(1,0,0)
         y_add(0,1,1,"g")
-        store(0,1,0)
-        u_int(3,0,"s")
-        h_use(2,0,0)
-        k_quant(3,0,0)
+        store(1,1,0)
         k_turn(3,1,0,"ss")
-        u_q(3,1)
-        u_q(3,0)
+        v_use(3,1,0)
+        h_use(2,1,1)
+        v_use(3,0,0)
         h_mm(2,1,0)
-        h_mm(3,0,1)
+        h_use(2,1,0)
+        u_int(3,0,"s")
+        k_quant(3,1,1)
+        v_use(3,1,1)
+        load_one_k(3,0,1)
+        h_mm(2,0,1)
+        u_int(3,1,"s")
+        y_add(2,1,1,"g")
+        h_use(2,0,1)
         k_quant(3,1,0)
         store(0,1,1)
-        k_quant(3,1,1)
-        h_mm(3,0,0)
-        h_mm(3,1,1)
         store(1,0,1)
-        h_use(2,1,0)
-        y_add(2,0,0,"g")
-        h_use(3,0,1)
-        y_add(2,1,0,"v")
-        h_use(3,0,0)
-        h_mm(2,0,1)
-        store(2,0,0)
-        y_add(3,0,1,"g")
-        h_use(3,1,1)
-        y_add(3,0,0,"v")
+        u_q(3,0)
+        store(1,0,0)
+        u_q(3,1)
+        h_mm(2,0,0)
+        store(2,1,1)
+        k_turn(3,0,1,"ss")
+        y_add(2,1,0,"g")
+        store(0,1,0)
         store(2,1,0)
-        h_mm(3,1,0)
-        h_use(2,0,1)
-        h_use(3,1,0)
-        store(0,0,1)
         y_add(2,0,1,"v")
-        y_add(3,1,1,"g")
-        store(3,0,1)
-        store(3,0,0)
-        store(3,1,1)
-        y_add(3,1,0,"v")
+        h_use(2,0,0)
+        y_add(2,0,0,"g")
+        h_mm(3,1,0)
+        k_quant(3,0,1)
+        k_quant(3,0,0)
+        h_mm(3,1,1)
+        h_mm(3,0,1)
+        store(1,1,1)
+        h_use(3,1,0)
+        h_use(3,1,1)
         store(2,0,1)
+        store(0,0,0)
+        y_add(3,1,0,"v")
+        store(2,0,0)
+        h_mm(3,0,0)
+        h_use(3,0,1)
+        y_add(3,1,1,"g")
+        h_use(3,0,0)
+        y_add(3,0,1,"v")
         store(3,1,0)
+        store(3,1,1)
+        store(3,0,1)
+        y_add(3,0,0,"v")
+        store(3,0,0)

@@ -27,7 +27,8 @@ def tile_step_weighted_time_kernel_f4_kernel(
     nc = tc.nc
 
     with ExitStack() as ctx:
-        raw_pool = ctx.enter_context(tc.tile_pool(name="raw", bufs=11))
+        raw_pool = ctx.enter_context(tc.tile_pool(name="raw", bufs=9))
+        wide_pool = ctx.enter_context(tc.tile_pool(name="wide", bufs=2))
         grp_pool = ctx.enter_context(tc.tile_pool(name="grp", bufs=5))
         keep = ctx.enter_context(tc.tile_pool(name="keep", bufs=1))
         kc_pool = ctx.enter_context(tc.tile_pool(name="kc", bufs=12))
@@ -84,29 +85,27 @@ def tile_step_weighted_time_kernel_f4_kernel(
                     out=out_ap, in0=in_ap, scalar1=1.0, scalar2=0.0, op0=ALU.mult, op1=ALU.add
                 )
 
-        def new_groups():
-            pair = []
-            for kp in range(2):
-                grp = grp_pool.tile([P, 2048], BF16, name="grp", align_bytes=64)
-                pair.append(grp)
-            return pair
-
-        def turn(raw, half, groups, engs):
+        def t_pe(key, raw, half, kp):
             words = raw[:].rearrange("p t k -> p (t k)").bitcast(F32)
-            for kp in range(2):
-                bank = tr_psum.tile([P, 2, 2, P], F32, name="bank")
-                for tt in range(2):
-                    for u in range(2):
-                        first = tt * 512 + 256 * kp + u
-                        nc.tensor.transpose(
-                            bank[:, tt, u, :], words[:, first : tt * 512 + 256 * (kp + 1) : 2], ident[:]
-                        )
-                dst = groups[kp][:].bitcast(F32)[:, 512 * half : 512 * (half + 1)]
-                copy(
-                    engs[kp],
-                    dst.rearrange("p (t r u) -> p t r u", t=2, u=2),
-                    bank[:].rearrange("p t u r -> p t r u"),
-                )
+            bank = tr_psum.tile([P, 2, 2, P], F32, name="bank")
+            for tt in range(2):
+                for u in range(2):
+                    first = tt * 512 + 256 * kp + u
+                    nc.tensor.transpose(
+                        bank[:, tt, u, :], words[:, first : tt * 512 + 256 * (kp + 1) : 2], ident[:]
+                    )
+            tbank[key, half, kp] = bank
+
+        def t_cp(key, half, kp, eng):
+            if (key, kp) not in groups_of:
+                grp = grp_pool.tile([P, 2048], BF16, name="grp", align_bytes=64)
+                groups_of[key, kp] = grp
+            dst = groups_of[key, kp][:].bitcast(F32)[:, 512 * half : 512 * (half + 1)]
+            copy(
+                eng,
+                dst.rearrange("p (t r u) -> p t r u", t=2, u=2),
+                tbank[key, half, kp][:].rearrange("p t u r -> p t r u"),
+            )
 
         def quantize(grp, pool, name):
             width = grp.shape[1] // PACK
@@ -183,13 +182,16 @@ def tile_step_weighted_time_kernel_f4_kernel(
         sm = keep.tile([P, PACK, 10], F32, name="sm")
         bc = keep.tile([P, 3, N], BF16, name="bc")
 
-        def prep_cols():
+        def cols_pe():
             bank = tr_psum.tile([P, PACK, P], BF16, name="bank")
             for t in range(PACK):
                 nc.tensor.transpose(bank[:, t, :], rows[:, t : K_PASS : PACK], ident_b[:])
-            nc.vector.tensor_copy(out=sm[:], in_=bank[:, :, 0:10])
+            tbank["cols"] = bank
 
-        def spread(r, eng):
+        def cols_cp():
+            nc.vector.tensor_copy(out=sm[:], in_=tbank["cols"][:, :, 0:10])
+
+        def spread_pe(r):
             bank = acc_psum.tile([P, N], BF16, name="acc")
             for nh in range(2):
                 nc.tensor.matmul(
@@ -199,8 +201,13 @@ def tile_step_weighted_time_kernel_f4_kernel(
                     start=True,
                     stop=True,
                 )
-            copy(eng, bc[:, r, :], bank[:])
+            tbank["spread", r] = bank
 
+        def spread_cp(r, eng):
+            copy(eng, bc[:, r, :], tbank["spread", r][:])
+
+        groups_of = {}
+        tbank = {}
         qx = {}
         qw = {}
         qk = {}
@@ -211,20 +218,6 @@ def tile_step_weighted_time_kernel_f4_kernel(
             for nh in range(2):
                 a[lg, nh] = keep.tile([P, PACK, 512], F32, name="a%d%d" % (lg, nh))
                 sg[lg, nh] = keep.tile([P, PACK, 512], F32, name="sg%d%d" % (lg, nh))
-
-        def prep_x(g, engs):
-            groups = new_groups()
-            for half in range(2):
-                turn(rx[g, half], half, groups, engs)
-            for kp in range(2):
-                qx[g, kp] = quantize(groups[kp], keep, "qx%d%d" % (g, kp))
-
-        def prep_k(j, g, engs):
-            groups = new_groups()
-            for half in range(2):
-                turn(rk[j, g, half], half, groups, engs)
-            for kp in range(2):
-                qk[j, g, kp] = quantize(groups[kp], kc_pool, "qk")
 
         def g_mm(lg, nh, t):
             acc = acc_psum.tile([P, 512], F32, name="acc")
@@ -269,13 +262,12 @@ def tile_step_weighted_time_kernel_f4_kernel(
                     mx(acc[:, tt, :], qx[lg, kp], (2 * tp + tt) * P, qw["i", j // 2, kp], (j % 2) * C, C, kp == 0, kp == 1)
             vacc[j, lg, tp] = acc
 
-        def v_use(j, lg, tp):
+        def u_mul(j, lg, tp):
             acc = vacc[j, lg, tp]
-            m = sg[lg, j // 2][:, :, cols_of(j)]
-            av = a[lg, j // 2][:, :, cols_of(j)]
             if (j, lg) not in ub_of:
                 ub = ub_pool.tile([P, PACK, C], BF16, name="ub", align_bytes=64)
                 ub_of[j, lg] = ub
+            m = sg[lg, j // 2][:, :, cols_of(j)]
             for tt in range(2):
                 t = 2 * tp + tt
                 nc.vector.scalar_tensor_tensor(
@@ -286,9 +278,11 @@ def tile_step_weighted_time_kernel_f4_kernel(
                     op0=ALU.mult,
                     op1=ALU.mult,
                 )
+
+        def v_dv(j, lg, tp):
             nc.vector.tensor_tensor(
-                out=av[:, 2 * tp : 2 * tp + 2, :],
-                in0=acc[:],
+                out=a[lg, j // 2][:, 2 * tp : 2 * tp + 2, cols_of(j)],
+                in0=vacc[j, lg, tp][:],
                 in1=bc[:, 2, j * C : (j + 1) * C].unsqueeze(1).to_broadcast([P, 2, C]),
                 op=ALU.mult,
             )
@@ -334,20 +328,20 @@ def tile_step_weighted_time_kernel_f4_kernel(
                 out=view[:, 2 * tp : 2 * tp + 2, :], in_=sg[g, j // 2][:, 2 * tp : 2 * tp + 2, cols_of(j)]
             )
 
-        groups_of = {}
+        def k_pe(j, g, half, kp):
+            t_pe((j, g), rk[j, g, half], half, kp)
 
-        def k_turn(j, g, half, engs):
-            if (j, g) not in groups_of:
-                groups_of[j, g] = new_groups()
-            turn(rk[j, g, half], half, groups_of[j, g], engs)
+        def k_cp(j, g, half, kp, eng):
+            t_cp((j, g), half, kp, eng)
 
         def k_quant(j, g, kp):
-            qk[j, g, kp] = quantize(groups_of[j, g][kp], kc_pool, "qk")
+            qk[j, g, kp] = quantize(groups_of[(j, g), kp], kc_pool, "qk")
 
-        def x_turn(g, half, engs):
-            if ("x", g) not in groups_of:
-                groups_of["x", g] = new_groups()
-            turn(rx[g, half], half, groups_of["x", g], engs)
+        def x_pe(g, half, kp):
+            t_pe(("x", g), rx[g, half], half, kp)
+
+        def x_cp(g, half, kp, eng):
+            t_cp(("x", g), half, kp, eng)
 
         for g in range(2):
             for kp in range(2):
@@ -356,9 +350,17 @@ def tile_step_weighted_time_kernel_f4_kernel(
                     qw["s", 0, kp] = new_planes(keep, "qws0%d" % kp)
 
         wgrp = {}
+        wide = {}
+
+        def load_wide(kp, jp):
+            if kp not in wide:
+                raw = wide_pool.tile([P, PACK, N], BF16, name="wide", align_bytes=64)
+                wide[kp] = raw
+            view = w_in[kp * K_PASS : (kp + 1) * K_PASS, :].rearrange("(p j) n -> p j n", j=PACK)
+            nc.sync.dma_start(out=wide[kp][:, 2 * jp : 2 * jp + 2, :], in_=view[:, 2 * jp : 2 * jp + 2, :])
 
         def x_quant(g, kp, half):
-            quantize_half(groups_of["x", g][kp], half, qx[g, kp])
+            quantize_half(groups_of[("x", g), kp], half, qx[g, kp])
 
         def load_first(kp, half):
             rw["s", 0, kp, half] = load_w_part(w_step, kp, 256 * half)
@@ -372,278 +374,369 @@ def tile_step_weighted_time_kernel_f4_kernel(
         def first_quant(kp, half):
             quantize_half(wgrp["s", 0, kp], half, qw["s", 0, kp])
 
-        def w_int(tag, nh, kp, eng):
-            grp = grp_pool.tile([P, 2048], BF16, name="grp", align_bytes=64)
-            interleave(eng, grp[:], rw[tag, nh, kp])
-            wgrp[tag, nh, kp] = grp
+        def w_int(tag, nh, kp, half, eng):
+            if (tag, nh, kp) not in wgrp:
+                grp = grp_pool.tile([P, 2048], BF16, name="grp", align_bytes=64)
+                wgrp[tag, nh, kp] = grp
+            if tag == "i":
+                c0 = 512 * nh + 256 * half
+                raw = wide[kp][:, :, c0 : c0 + 256]
+            else:
+                raw = rw[tag, nh, kp][:, :, 256 * half : 256 * (half + 1)]
+            interleave(eng, wgrp[tag, nh, kp][:, 1024 * half : 1024 * (half + 1)], raw)
 
         def w_quant(tag, nh, kp):
             qw[tag, nh, kp] = quantize(wgrp[tag, nh, kp], keep, "qw%s%d%d" % (tag, nh, kp))
 
-
-        load_first(1,0)
+        load_first(0,1)
         load_one_x(1,1)
-        load_one_x(1,0)
-        x_turn(1,1,"vv")
-        load_first(1,1)
+        x_pe(1,1,1)
+        x_pe(1,1,0)
+        first_int(0,1,"v")
         load_first(0,0)
         first_int(0,0,"s")
-        first_int(1,0,"g")
-        load_first(0,1)
-        first_int(1,1,"g")
-        first_quant(1,0)
-        spread(2,"v")
-        first_quant(1,1)
-        x_quant(1,1,1)
-        load_one_x(0,1)
-        first_int(0,1,"v")
-        first_quant(0,0)
-        x_turn(1,0,"ss")
-        load_one_x(0,0)
-        x_quant(1,0,1)
-        load_one_w(w_step,"s",1,1)
-        load_one_w(w_step,"s",1,0)
-        spread(0,"s")
-        x_turn(0,1,"ss")
-        x_turn(0,0,"ss")
-        w_int("s",1,0,"s")
-        load_one_w(w_in,"i",1,1)
-        x_quant(1,0,0)
-        x_quant(1,1,0)
-        load_one_w(w_in,"i",0,1)
+        load_one_x(1,0)
+        x_cp(1,1,0,"s")
         first_quant(0,1)
-        g_mm(1,0,1)
-        x_quant(0,0,1)
-        w_int("s",1,1,"v")
-        w_int("i",0,1,"s")
-        x_quant(0,0,0)
-        x_quant(0,1,1)
-        g_mm(0,0,2)
+        load_first(1,1)
+        x_cp(1,1,1,"v")
+        x_quant(1,1,1)
+        spread_pe(2)
+        load_first(1,0)
+        first_quant(0,0)
+        x_pe(1,0,1)
+        first_int(1,1,"s")
+        x_quant(1,0,1)
+        load_one_x(0,1)
+        x_pe(1,0,0)
+        first_int(1,0,"v")
+        load_one_w(w_step,"s",1,1)
+        first_quant(1,0)
+        x_cp(1,0,1,"s")
+        x_quant(1,1,0)
+        x_cp(1,0,0,"s")
+        x_quant(1,0,0)
+        first_quant(1,1)
+        spread_pe(0)
+        spread_cp(0,"s")
+        x_pe(0,1,1)
+        w_int("s",1,1,1,"s")
+        spread_cp(2,"s")
+        x_cp(0,1,1,"v")
+        x_pe(0,1,0)
+        x_cp(0,1,0,"v")
+        w_int("s",1,1,0,"g")
         g_mm(1,0,2)
-        w_quant("s",1,1)
-        load_one_w(w_in,"i",0,0)
-        g_mm(0,0,3)
-        g_use(1,0,1)
-        load_one_k(0,0,1)
-        g_use(0,0,2)
         g_use(1,0,2)
-        g_mm(1,0,0)
-        load_one_k(1,0,0)
-        g_use(0,0,3)
-        sig(0,0,1)
-        load_one_k(1,1,1)
-        g_use(1,0,0)
-        prep_cols()
-        x_quant(0,1,0)
-        w_quant("s",1,0)
+        load_one_x(0,0)
+        x_pe(0,0,0)
+        x_pe(0,0,1)
+        x_quant(0,0,1)
+        x_quant(0,1,1)
+        load_one_w(w_step,"s",1,0)
         g_mm(1,0,3)
-        load_one_w(w_in,"i",1,0)
-        g_mm(0,0,1)
+        w_quant("s",1,1)
+        x_cp(0,0,0,"s")
+        x_quant(0,0,0)
+        g_mm(1,0,0)
         g_use(1,0,3)
-        g_mm(0,1,3)
-        g_use(0,0,1)
-        g_mm(0,0,0)
-        w_int("i",1,1,"g")
-        load_one_k(0,1,0)
-        g_use(0,1,3)
-        g_use(0,0,0)
-        g_mm(0,1,1)
-        sig(1,0,0)
+        g_use(1,0,0)
+        w_int("s",1,0,1,"g")
+        g_mm(0,0,2)
+        g_use(0,0,2)
+        x_cp(0,0,1,"s")
+        x_quant(0,1,0)
+        g_mm(1,0,1)
+        load_one_k(0,0,0)
+        w_int("s",1,0,0,"s")
+        g_mm(0,0,3)
+        w_quant("s",1,0)
+        g_use(1,0,1)
+        g_use(0,0,3)
         sig(1,0,1)
+        cols_pe()
+        g_mm(0,0,0)
+        g_use(0,0,0)
+        load_wide(0,0)
+        g_mm(1,1,0)
+        g_use(1,1,0)
+        load_wide(0,1)
+        cols_cp()
+        g_mm(0,0,1)
+        g_mm(1,1,2)
+        g_use(0,0,1)
+        g_mm(0,1,0)
+        g_use(1,1,2)
+        w_int("i",0,0,0,"s")
+        g_use(0,1,0)
+        load_wide(1,1)
+        w_int("i",1,0,1,"g")
+        g_mm(0,1,2)
+        g_use(0,1,2)
+        load_wide(1,0)
+        w_int("i",0,1,1,"g")
+        g_mm(0,1,1)
+        g_use(0,1,1)
+        g_mm(0,1,3)
+        g_use(0,1,3)
+        sig(1,0,0)
+        load_one_k(1,0,0)
+        g_mm(1,1,1)
+        g_use(1,1,1)
+        g_mm(1,1,3)
+        g_use(1,1,3)
+        sig(0,0,1)
+        w_int("i",0,1,0,"g")
+        w_quant("i",0,1)
         sig(0,0,0)
         ln(1,1)
-        g_mm(0,1,0)
-        w_int("i",0,0,"g")
-        g_use(0,1,1)
-        g_mm(0,1,2)
-        w_quant("i",1,1)
-        ln(1,0)
-        ln(0,0)
-        load_one_k(1,0,1)
+        w_int("i",0,0,1,"g")
         w_quant("i",0,0)
-        g_use(0,1,0)
-        w_int("i",1,0,"g")
-        g_mm(1,1,3)
-        g_use(0,1,2)
-        load_one_k(2,1,1)
-        g_mm(1,1,1)
-        g_use(1,1,3)
-        g_use(1,1,1)
-        load_one_k(2,0,1)
-        g_mm(1,1,0)
-        load_one_k(1,1,0)
-        load_one_k(0,0,0)
-        g_use(1,1,0)
-        k_turn(1,0,0,"ss")
-        w_quant("i",0,1)
-        w_quant("i",1,0)
-        load_one_k(0,1,1)
-        v_mm(1,1,0)
-        v_mm(1,1,1)
         m_max(1,1)
-        v_mm(1,0,0)
-        m_max(1,0)
-        load_one_k(3,1,1)
+        w_int("i",1,0,0,"s")
+        w_quant("i",1,0)
+        v_mm(1,1,1)
+        u_mul(1,1,1)
         ln(0,1)
-        v_use(1,1,0)
-        k_turn(1,0,1,"ss")
-        sig(1,1,0)
-        v_mm(0,0,1)
-        load_one_k(2,0,0)
-        m_max(0,0)
-        v_use(1,1,1)
-        v_mm(1,0,1)
-        g_mm(1,1,2)
-        k_turn(1,1,1,"ss")
-        v_use(1,0,0)
-        u_int(1,1,"g")
-        v_use(1,0,1)
-        g_use(1,1,2)
-        v_use(0,0,1)
-        k_turn(1,1,0,"ss")
-        u_int(1,0,"g")
+        v_mm(1,1,0)
         m_max(0,1)
-        u_q(1,1)
-        sig(0,1,0)
-        v_mm(0,0,0)
-        u_q(1,0)
-        sig(1,1,1)
-        v_mm(0,1,1)
-        k_quant(1,0,0)
-        spread(1,"s")
-        k_quant(1,0,1)
-        v_use(0,0,0)
-        sig(0,1,1)
-        h_mm(1,0,1)
-        ln(2,1)
-        v_use(0,1,1)
-        h_use(1,0,1)
-        k_quant(1,1,0)
-        k_turn(0,0,0,"ss")
-        h_mm(1,0,0)
+        u_mul(1,1,0)
+        ln(1,0)
+        v_dv(1,1,0)
+        u_int(1,1,"g")
+        ln(0,0)
+        v_dv(1,1,1)
         v_mm(0,1,0)
-        k_quant(1,1,1)
-        h_mm(1,1,1)
-        v_mm(2,1,1)
-        k_turn(0,0,1,"ss")
-        v_use(0,1,0)
-        h_use(1,0,0)
-        u_int(0,1,"s")
-        u_int(0,0,"g")
-        v_mm(2,1,0)
-        k_turn(0,1,0,"ss")
-        ln(2,0)
-        y_add(1,0,1,"g")
-        h_mm(1,1,0)
-        m_max(2,1)
-        k_turn(0,1,1,"ss")
-        h_use(1,1,1)
-        v_use(2,1,1)
-        v_use(2,1,0)
-        y_add(1,0,0,"g")
+        u_mul(0,1,0)
+        v_dv(0,1,0)
+        m_max(0,0)
+        k_pe(1,0,0,0)
+        v_mm(0,1,1)
+        u_mul(0,1,1)
+        m_max(1,0)
+        v_mm(0,0,0)
+        load_one_k(0,0,1)
+        k_pe(0,0,1,0)
+        v_dv(0,1,1)
+        u_mul(0,0,0)
+        v_dv(0,0,0)
+        v_mm(1,0,0)
+        v_dv(1,0,0)
+        k_cp(1,0,0,0,"s")
+        u_int(0,1,"g")
+        k_pe(0,0,1,1)
+        sig(0,1,1)
+        v_mm(1,0,1)
+        u_mul(1,0,1)
+        v_mm(0,0,1)
+        v_dv(0,0,1)
+        v_dv(1,0,1)
+        load_one_k(1,0,1)
+        w_int("i",1,1,1,"g")
+        k_pe(1,0,1,0)
+        u_mul(1,0,0)
+        sig(1,1,1)
+        u_mul(0,0,1)
+        sig(0,1,0)
+        k_pe(0,0,0,1)
+        k_cp(0,0,1,0,"s")
+        sig(1,1,0)
+        k_pe(1,0,0,1)
+        k_cp(0,0,1,1,"s")
         u_q(0,1)
+        u_q(1,1)
+        spread_pe(1)
+        w_int("i",1,1,0,"g")
+        w_quant("i",1,1)
+        ln(2,1)
+        m_max(2,1)
+        u_int(0,0,"g")
+        k_cp(1,0,1,0,"s")
+        k_quant(1,0,0)
+        v_mm(2,1,0)
+        u_mul(2,1,0)
+        v_dv(2,1,0)
+        k_cp(0,0,0,1,"s")
+        spread_cp(1,"s")
+        v_mm(2,1,1)
+        u_mul(2,1,1)
+        u_int(1,0,"s")
+        u_q(1,0)
+        load_one_k(1,1,0)
+        k_pe(0,0,0,0)
+        k_pe(1,0,1,1)
+        k_cp(1,0,0,1,"s")
         k_quant(0,0,1)
-        u_int(2,1,"s")
-        load_one_k(3,0,0)
-        h_use(1,1,0)
-        u_q(0,0)
-        v_mm(2,0,0)
+        k_cp(1,0,1,1,"s")
+        k_quant(1,0,1)
+        k_cp(0,0,0,0,"s")
         k_quant(0,0,0)
-        k_quant(0,1,0)
-        k_turn(2,0,1,"ss")
-        ln(3,0)
-        ln(3,1)
-        y_add(1,1,1,"g")
-        h_mm(0,0,1)
+        ln(2,0)
         v_mm(2,0,1)
+        v_dv(2,1,1)
+        k_pe(1,1,0,0)
+        v_mm(2,0,0)
+        h_mm(1,0,0)
+        load_one_k(1,1,1)
+        k_pe(1,1,1,0)
+        ln(3,0)
+        u_q(0,0)
+        h_use(1,0,0)
+        k_cp(1,1,0,0,"s")
         m_max(2,0)
-        load_one_k(3,1,0)
-        h_use(0,0,1)
-        k_quant(0,1,1)
-        v_mm(3,0,1)
-        v_use(2,0,0)
-        v_use(2,0,1)
-        y_add(0,0,1,"g")
-        k_turn(2,1,1,"ss")
-        h_mm(0,1,0)
-        y_add(1,1,0,"g")
+        k_pe(1,1,0,1)
         h_mm(0,0,0)
-        h_use(0,1,0)
-        v_mm(3,1,0)
-        u_int(2,0,"s")
-        load_one_k(2,1,0)
-        u_q(2,1)
-        m_max(3,0)
-        h_mm(0,1,1)
-        k_turn(2,0,0,"ss")
-        m_max(3,1)
-        v_use(3,0,1)
-        v_mm(3,1,1)
-        k_turn(2,1,0,"ss")
+        load_one_k(2,1,1)
         h_use(0,0,0)
+        h_mm(0,0,1)
+        u_mul(2,0,0)
+        h_use(0,0,1)
+        k_pe(1,1,1,1)
+        load_one_k(0,1,1)
+        load_one_k(0,1,0)
+        k_pe(0,1,0,0)
+        k_pe(0,1,1,0)
+        k_cp(1,1,0,1,"s")
+        k_cp(1,1,1,0,"s")
+        u_int(2,1,"s")
+        u_mul(2,0,1)
+        v_dv(2,0,0)
+        load_one_k(3,0,1)
+        v_dv(2,0,1)
+        k_cp(0,1,0,0,"s")
+        k_cp(1,1,1,1,"s")
+        h_mm(1,0,1)
+        h_use(1,0,1)
+        load_one_k(2,0,1)
+        y_add(1,0,0,"g")
+        u_int(2,0,"s")
+        k_quant(1,1,1)
+        k_quant(1,1,0)
+        v_mm(3,0,1)
+        k_cp(0,1,1,0,"s")
+        u_q(2,1)
         u_q(2,0)
+        k_pe(0,1,0,1)
+        k_quant(0,1,0)
+        k_cp(0,1,0,1,"s")
         v_mm(3,0,0)
-        store(0,0,1)
-        k_quant(2,1,0)
-        k_turn(3,0,0,"ss")
-        k_quant(2,1,1)
-        y_add(0,1,0,"g")
-        h_mm(2,1,1)
-        k_turn(3,1,1,"ss")
+        k_pe(0,1,1,1)
+        m_max(3,0)
         y_add(0,0,0,"g")
+        k_cp(0,1,1,1,"s")
+        load_one_k(2,1,0)
+        load_one_k(3,1,1)
+        k_quant(0,1,1)
+        k_pe(2,1,0,1)
+        k_cp(2,1,0,1,"s")
+        u_mul(3,0,1)
+        k_pe(2,0,1,1)
+        h_mm(1,1,0)
+        k_cp(2,0,1,1,"s")
+        h_use(1,1,0)
+        load_one_k(3,1,0)
+        v_dv(3,0,1)
+        y_add(0,0,1,"g")
+        ln(3,1)
+        load_one_k(2,0,0)
+        k_pe(2,0,0,0)
+        k_pe(2,0,0,1)
+        u_mul(3,0,0)
+        h_mm(0,1,0)
+        k_cp(2,0,0,0,"s")
+        h_use(0,1,0)
+        k_cp(2,0,0,1,"s")
+        m_max(3,1)
+        k_pe(2,0,1,0)
+        k_cp(2,0,1,0,"s")
         k_quant(2,0,0)
+        k_pe(2,1,1,0)
+        k_pe(2,1,0,0)
         k_quant(2,0,1)
+        v_mm(3,1,1)
+        k_cp(2,1,0,0,"s")
+        k_pe(2,1,1,1)
+        k_pe(3,1,0,0)
+        y_add(1,0,1,"g")
+        store(1,0,1)
+        k_cp(2,1,1,0,"s")
+        k_quant(2,1,0)
+        k_cp(2,1,1,1,"s")
+        k_quant(2,1,1)
+        h_mm(1,1,1)
+        h_use(1,1,1)
+        y_add(1,1,0,"g")
+        h_mm(0,1,1)
         h_use(0,1,1)
-        y_add(0,1,1,"g")
-        store(1,1,0)
-        k_turn(3,1,0,"ss")
-        v_use(3,1,0)
-        h_use(2,1,1)
-        v_use(3,0,0)
+        v_mm(3,1,0)
+        v_dv(3,1,0)
+        u_mul(3,1,0)
+        u_int(3,0,"s")
         h_mm(2,1,0)
         h_use(2,1,0)
-        u_int(3,0,"s")
-        k_quant(3,1,1)
-        v_use(3,1,1)
-        load_one_k(3,0,1)
-        h_mm(2,0,1)
-        u_int(3,1,"s")
-        y_add(2,1,1,"g")
-        h_use(2,0,1)
-        k_quant(3,1,0)
-        store(0,1,1)
-        store(1,0,1)
-        u_q(3,0)
-        store(1,0,0)
-        u_q(3,1)
+        u_mul(3,1,1)
+        v_dv(3,1,1)
+        k_pe(3,1,1,1)
+        v_dv(3,0,0)
         h_mm(2,0,0)
-        store(2,1,1)
-        k_turn(3,0,1,"ss")
-        y_add(2,1,0,"g")
-        store(0,1,0)
-        store(2,1,0)
-        y_add(2,0,1,"v")
         h_use(2,0,0)
-        y_add(2,0,0,"g")
-        h_mm(3,1,0)
-        k_quant(3,0,1)
-        k_quant(3,0,0)
-        h_mm(3,1,1)
-        h_mm(3,0,1)
-        store(1,1,1)
-        h_use(3,1,0)
-        h_use(3,1,1)
-        store(2,0,1)
+        k_cp(3,1,0,0,"s")
+        y_add(0,1,0,"g")
+        u_q(3,0)
+        k_pe(3,1,0,1)
+        k_cp(3,1,0,1,"s")
+        k_pe(3,1,1,0)
+        y_add(1,1,1,"g")
+        k_cp(3,1,1,1,"s")
+        k_quant(3,1,1)
+        h_mm(2,1,1)
+        k_cp(3,1,1,0,"s")
+        y_add(0,1,1,"g")
+        store(1,0,0)
+        load_one_k(3,0,0)
+        u_int(3,1,"s")
+        k_pe(3,0,0,0)
         store(0,0,0)
-        y_add(3,1,0,"v")
+        store(1,1,1)
+        y_add(2,1,0,"g")
+        y_add(2,0,0,"g")
+        k_quant(3,1,0)
+        h_use(2,1,1)
+        k_cp(3,0,0,0,"s")
+        k_pe(3,0,1,0)
+        k_cp(3,0,1,0,"s")
         store(2,0,0)
-        h_mm(3,0,0)
+        h_mm(2,0,1)
+        h_use(2,0,1)
+        k_pe(3,0,0,1)
+        k_pe(3,0,1,1)
+        u_q(3,1)
+        h_mm(3,1,1)
+        store(2,1,0)
+        k_cp(3,0,0,1,"s")
+        y_add(2,1,1,"v")
+        store(2,1,1)
+        k_quant(3,0,0)
+        store(0,0,1)
+        h_mm(3,1,0)
+        k_cp(3,0,1,1,"s")
+        k_quant(3,0,1)
+        h_mm(3,0,1)
+        y_add(2,0,1,"g")
+        h_use(3,1,1)
+        h_use(3,1,0)
+        y_add(3,1,0,"g")
+        y_add(3,1,1,"v")
         h_use(3,0,1)
-        y_add(3,1,1,"g")
+        store(0,1,1)
+        store(1,1,0)
+        store(0,1,0)
+        store(2,0,1)
+        h_mm(3,0,0)
         h_use(3,0,0)
         y_add(3,0,1,"v")
-        store(3,1,0)
         store(3,1,1)
+        store(3,1,0)
         store(3,0,1)
         y_add(3,0,0,"v")
         store(3,0,0)

@@ -27,8 +27,7 @@ def tile_step_weighted_time_kernel_f4_kernel(
     nc = tc.nc
 
     with ExitStack() as ctx:
-        raw_pool = ctx.enter_context(tc.tile_pool(name="raw", bufs=9))
-        wide_pool = ctx.enter_context(tc.tile_pool(name="wide", bufs=2))
+        raw_pool = ctx.enter_context(tc.tile_pool(name="raw", bufs=11))
         grp_pool = ctx.enter_context(tc.tile_pool(name="grp", bufs=5))
         keep = ctx.enter_context(tc.tile_pool(name="keep", bufs=1))
         kc_pool = ctx.enter_context(tc.tile_pool(name="kc", bufs=12))
@@ -350,14 +349,6 @@ def tile_step_weighted_time_kernel_f4_kernel(
                     qw["s", 0, kp] = new_planes(keep, "qws0%d" % kp)
 
         wgrp = {}
-        wide = {}
-
-        def load_wide(kp, jp):
-            if kp not in wide:
-                raw = wide_pool.tile([P, PACK, N], BF16, name="wide", align_bytes=64)
-                wide[kp] = raw
-            view = w_in[kp * K_PASS : (kp + 1) * K_PASS, :].rearrange("(p j) n -> p j n", j=PACK)
-            nc.sync.dma_start(out=wide[kp][:, 2 * jp : 2 * jp + 2, :], in_=view[:, 2 * jp : 2 * jp + 2, :])
 
         def x_quant(g, kp, half):
             quantize_half(groups_of[("x", g), kp], half, qx[g, kp])
@@ -374,369 +365,357 @@ def tile_step_weighted_time_kernel_f4_kernel(
         def first_quant(kp, half):
             quantize_half(wgrp["s", 0, kp], half, qw["s", 0, kp])
 
-        def w_int(tag, nh, kp, half, eng):
-            if (tag, nh, kp) not in wgrp:
-                grp = grp_pool.tile([P, 2048], BF16, name="grp", align_bytes=64)
-                wgrp[tag, nh, kp] = grp
-            if tag == "i":
-                c0 = 512 * nh + 256 * half
-                raw = wide[kp][:, :, c0 : c0 + 256]
-            else:
-                raw = rw[tag, nh, kp][:, :, 256 * half : 256 * (half + 1)]
-            interleave(eng, wgrp[tag, nh, kp][:, 1024 * half : 1024 * (half + 1)], raw)
+        def w_int(tag, nh, kp, eng):
+            grp = grp_pool.tile([P, 2048], BF16, name="grp", align_bytes=64)
+            interleave(eng, grp[:], rw[tag, nh, kp])
+            wgrp[tag, nh, kp] = grp
 
         def w_quant(tag, nh, kp):
             qw[tag, nh, kp] = quantize(wgrp[tag, nh, kp], keep, "qw%s%d%d" % (tag, nh, kp))
 
-        load_first(0,1)
-        load_one_x(1,1)
-        x_pe(1,1,1)
-        x_pe(1,1,0)
-        first_int(0,1,"v")
-        load_first(0,0)
-        first_int(0,0,"s")
         load_one_x(1,0)
-        x_cp(1,1,0,"s")
-        first_quant(0,1)
-        load_first(1,1)
-        x_cp(1,1,1,"v")
-        x_quant(1,1,1)
-        spread_pe(2)
         load_first(1,0)
-        first_quant(0,0)
-        x_pe(1,0,1)
-        first_int(1,1,"s")
-        x_quant(1,0,1)
-        load_one_x(0,1)
-        x_pe(1,0,0)
         first_int(1,0,"v")
-        load_one_w(w_step,"s",1,1)
-        first_quant(1,0)
+        load_first(0,1)
+        x_pe(1,0,1)
         x_cp(1,0,1,"s")
-        x_quant(1,1,0)
+        load_one_x(1,1)
+        x_pe(1,0,0)
+        first_int(0,1,"v")
+        load_first(1,1)
         x_cp(1,0,0,"s")
-        x_quant(1,0,0)
-        first_quant(1,1)
+        load_one_w(w_step,"s",1,1)
+        x_pe(1,1,1)
+        load_one_x(0,0)
+        load_first(0,0)
+        load_one_x(0,1)
+        load_one_w(w_in,"i",1,1)
+        x_quant(1,1,0)
+        x_cp(1,1,1,"s")
+        first_quant(0,1)
         spread_pe(0)
         spread_cp(0,"s")
-        x_pe(0,1,1)
-        w_int("s",1,1,1,"s")
+        x_pe(1,1,0)
+        x_quant(1,0,0)
+        load_one_w(w_step,"s",1,0)
+        spread_pe(2)
+        load_one_w(w_in,"i",0,1)
+        first_quant(1,0)
+        load_one_k(2,0,1)
+        x_cp(1,1,0,"s")
         spread_cp(2,"s")
-        x_cp(0,1,1,"v")
+        x_pe(0,0,1)
+        first_int(1,1,"v")
+        first_quant(1,1)
+        load_one_k(1,0,0)
+        w_int("s",1,1,"v")
+        x_cp(0,0,1,"s")
+        x_quant(1,1,1)
+        x_pe(0,0,0)
+        x_cp(0,0,0,"s")
+        w_quant("s",1,1)
+        first_int(0,0,"v")
+        first_quant(0,0)
+        x_quant(1,0,1)
+        x_quant(0,1,0)
         x_pe(0,1,0)
-        x_cp(0,1,0,"v")
-        w_int("s",1,1,0,"g")
+        load_one_w(w_in,"i",1,0)
+        x_cp(0,1,0,"s")
+        w_int("i",1,1,"s")
+        x_quant(0,0,0)
+        x_pe(0,1,1)
+        w_int("s",1,0,"s")
+        x_cp(0,1,1,"v")
+        g_mm(1,0,3)
+        x_quant(0,0,1)
+        load_one_w(w_in,"i",0,0)
+        x_quant(0,1,1)
+        g_mm(0,0,1)
+        g_use(1,0,3)
+        g_mm(0,0,0)
+        g_use(0,0,1)
+        g_use(0,0,0)
+        load_one_k(3,1,1)
+        g_mm(1,0,0)
+        g_use(1,0,0)
         g_mm(1,0,2)
         g_use(1,0,2)
-        load_one_x(0,0)
-        x_pe(0,0,0)
-        x_pe(0,0,1)
-        x_quant(0,0,1)
-        x_quant(0,1,1)
-        load_one_w(w_step,"s",1,0)
-        g_mm(1,0,3)
-        w_quant("s",1,1)
-        x_cp(0,0,0,"s")
-        x_quant(0,0,0)
-        g_mm(1,0,0)
-        g_use(1,0,3)
-        g_use(1,0,0)
-        w_int("s",1,0,1,"g")
+        g_mm(1,0,1)
+        g_use(1,0,1)
+        g_mm(0,0,3)
+        g_use(0,0,3)
+        w_int("i",0,1,"g")
+        cols_pe()
+        cols_cp()
+        sig(0,0,0)
+        w_quant("s",1,0)
+        sig(1,0,0)
+        w_quant("i",0,1)
+        w_quant("i",1,1)
         g_mm(0,0,2)
         g_use(0,0,2)
-        x_cp(0,0,1,"s")
-        x_quant(0,1,0)
-        g_mm(1,0,1)
-        load_one_k(0,0,0)
-        w_int("s",1,0,0,"s")
-        g_mm(0,0,3)
-        w_quant("s",1,0)
-        g_use(1,0,1)
-        g_use(0,0,3)
-        sig(1,0,1)
-        cols_pe()
-        g_mm(0,0,0)
-        g_use(0,0,0)
-        load_wide(0,0)
+        g_mm(0,1,0)
+        g_use(0,1,0)
         g_mm(1,1,0)
         g_use(1,1,0)
-        load_wide(0,1)
-        cols_cp()
-        g_mm(0,0,1)
-        g_mm(1,1,2)
-        g_use(0,0,1)
-        g_mm(0,1,0)
-        g_use(1,1,2)
-        w_int("i",0,0,0,"s")
-        g_use(0,1,0)
-        load_wide(1,1)
-        w_int("i",1,0,1,"g")
-        g_mm(0,1,2)
-        g_use(0,1,2)
-        load_wide(1,0)
-        w_int("i",0,1,1,"g")
         g_mm(0,1,1)
         g_use(0,1,1)
+        g_mm(1,1,2)
+        g_mm(1,1,3)
+        g_use(1,1,2)
+        load_one_k(3,0,1)
+        w_int("i",0,0,"g")
+        sig(1,0,1)
         g_mm(0,1,3)
+        g_use(1,1,3)
         g_use(0,1,3)
-        sig(1,0,0)
-        load_one_k(1,0,0)
+        load_one_k(0,0,0)
+        g_mm(0,1,2)
+        w_quant("i",0,0)
+        g_use(0,1,2)
+        sig(0,0,1)
+        ln(1,1)
         g_mm(1,1,1)
         g_use(1,1,1)
-        g_mm(1,1,3)
-        g_use(1,1,3)
-        sig(0,0,1)
-        w_int("i",0,1,0,"g")
-        w_quant("i",0,1)
-        sig(0,0,0)
-        ln(1,1)
-        w_int("i",0,0,1,"g")
-        w_quant("i",0,0)
         m_max(1,1)
-        w_int("i",1,0,0,"s")
-        w_quant("i",1,0)
         v_mm(1,1,1)
-        u_mul(1,1,1)
+        k_pe(1,0,0,1)
         ln(0,1)
-        v_mm(1,1,0)
         m_max(0,1)
-        u_mul(1,1,0)
-        ln(1,0)
+        v_mm(1,1,0)
         v_dv(1,1,0)
-        u_int(1,1,"g")
+        load_one_k(1,0,1)
+        u_mul(1,1,1)
+        u_mul(1,1,0)
+        k_pe(1,0,1,1)
+        k_pe(1,0,1,0)
+        v_mm(1,0,1)
+        k_pe(1,0,0,0)
+        load_one_k(0,1,0)
+        ln(1,0)
+        load_one_k(1,1,1)
+        k_pe(1,1,1,1)
         ln(0,0)
+        load_one_k(0,0,1)
+        m_max(1,0)
+        m_max(0,0)
+        k_cp(1,0,1,0,"s")
         v_dv(1,1,1)
+        u_mul(1,0,1)
+        v_dv(1,0,1)
+        v_mm(0,0,1)
+        u_mul(0,0,1)
+        v_dv(0,0,1)
         v_mm(0,1,0)
         u_mul(0,1,0)
         v_dv(0,1,0)
-        m_max(0,0)
-        k_pe(1,0,0,0)
-        v_mm(0,1,1)
-        u_mul(0,1,1)
-        m_max(1,0)
-        v_mm(0,0,0)
-        load_one_k(0,0,1)
-        k_pe(0,0,1,0)
-        v_dv(0,1,1)
-        u_mul(0,0,0)
-        v_dv(0,0,0)
+        u_int(1,1,"g")
+        k_pe(1,1,1,0)
+        load_one_k(0,1,1)
+        k_cp(1,0,1,1,"s")
         v_mm(1,0,0)
         v_dv(1,0,0)
-        k_cp(1,0,0,0,"s")
-        u_int(0,1,"g")
-        k_pe(0,0,1,1)
-        sig(0,1,1)
-        v_mm(1,0,1)
-        u_mul(1,0,1)
-        v_mm(0,0,1)
-        v_dv(0,0,1)
-        v_dv(1,0,1)
-        load_one_k(1,0,1)
-        w_int("i",1,1,1,"g")
-        k_pe(1,0,1,0)
+        k_cp(1,0,0,1,"s")
+        v_mm(0,1,1)
+        v_dv(0,1,1)
         u_mul(1,0,0)
-        sig(1,1,1)
-        u_mul(0,0,1)
+        w_int("i",1,0,"g")
+        w_quant("i",1,0)
+        u_mul(0,1,1)
         sig(0,1,0)
-        k_pe(0,0,0,1)
-        k_cp(0,0,1,0,"s")
+        u_int(1,0,"g")
         sig(1,1,0)
-        k_pe(1,0,0,1)
-        k_cp(0,0,1,1,"s")
-        u_q(0,1)
+        v_mm(0,0,0)
+        u_mul(0,0,0)
+        v_dv(0,0,0)
+        k_pe(0,1,0,0)
+        load_one_k(2,1,0)
+        load_one_k(1,1,0)
         u_q(1,1)
-        spread_pe(1)
-        w_int("i",1,1,0,"g")
-        w_quant("i",1,1)
-        ln(2,1)
-        m_max(2,1)
-        u_int(0,0,"g")
-        k_cp(1,0,1,0,"s")
+        k_cp(1,1,1,1,"s")
+        sig(0,1,1)
+        k_pe(1,1,0,0)
+        k_pe(1,1,0,1)
+        k_cp(1,0,0,0,"s")
         k_quant(1,0,0)
         v_mm(2,1,0)
-        u_mul(2,1,0)
-        v_dv(2,1,0)
-        k_cp(0,0,0,1,"s")
-        spread_cp(1,"s")
-        v_mm(2,1,1)
-        u_mul(2,1,1)
-        u_int(1,0,"s")
         u_q(1,0)
-        load_one_k(1,1,0)
-        k_pe(0,0,0,0)
-        k_pe(1,0,1,1)
-        k_cp(1,0,0,1,"s")
-        k_quant(0,0,1)
-        k_cp(1,0,1,1,"s")
         k_quant(1,0,1)
-        k_cp(0,0,0,0,"s")
-        k_quant(0,0,0)
-        ln(2,0)
-        v_mm(2,0,1)
-        v_dv(2,1,1)
-        k_pe(1,1,0,0)
-        v_mm(2,0,0)
-        h_mm(1,0,0)
-        load_one_k(1,1,1)
-        k_pe(1,1,1,0)
-        ln(3,0)
-        u_q(0,0)
-        h_use(1,0,0)
-        k_cp(1,1,0,0,"s")
-        m_max(2,0)
-        k_pe(1,1,0,1)
-        h_mm(0,0,0)
-        load_one_k(2,1,1)
-        h_use(0,0,0)
-        h_mm(0,0,1)
-        u_mul(2,0,0)
-        h_use(0,0,1)
-        k_pe(1,1,1,1)
-        load_one_k(0,1,1)
-        load_one_k(0,1,0)
-        k_pe(0,1,0,0)
-        k_pe(0,1,1,0)
-        k_cp(1,1,0,1,"s")
-        k_cp(1,1,1,0,"s")
-        u_int(2,1,"s")
-        u_mul(2,0,1)
-        v_dv(2,0,0)
-        load_one_k(3,0,1)
-        v_dv(2,0,1)
-        k_cp(0,1,0,0,"s")
-        k_cp(1,1,1,1,"s")
-        h_mm(1,0,1)
-        h_use(1,0,1)
-        load_one_k(2,0,1)
-        y_add(1,0,0,"g")
-        u_int(2,0,"s")
-        k_quant(1,1,1)
-        k_quant(1,1,0)
-        v_mm(3,0,1)
-        k_cp(0,1,1,0,"s")
-        u_q(2,1)
-        u_q(2,0)
-        k_pe(0,1,0,1)
-        k_quant(0,1,0)
-        k_cp(0,1,0,1,"s")
-        v_mm(3,0,0)
+        spread_pe(1)
+        sig(1,1,1)
         k_pe(0,1,1,1)
-        m_max(3,0)
-        y_add(0,0,0,"g")
+        v_mm(2,0,1)
+        k_cp(1,1,1,0,"s")
+        k_cp(1,1,0,0,"s")
+        ln(2,0)
+        k_quant(1,1,0)
+        m_max(2,0)
+        k_cp(1,1,0,1,"s")
+        k_quant(1,1,1)
+        h_mm(1,0,1)
+        h_mm(1,0,0)
+        load_one_k(3,1,0)
+        spread_cp(1,"s")
+        h_use(1,0,0)
+        v_mm(2,0,0)
+        u_mul(2,0,0)
+        h_use(1,0,1)
+        v_dv(2,0,0)
+        k_cp(0,1,0,0,"s")
+        u_mul(2,0,1)
+        v_dv(2,0,1)
+        k_pe(0,1,0,1)
+        k_pe(0,1,1,0)
+        h_mm(1,1,1)
+        h_use(1,1,1)
         k_cp(0,1,1,1,"s")
-        load_one_k(2,1,0)
-        load_one_k(3,1,1)
+        u_int(0,1,"s")
+        u_q(0,1)
+        k_cp(0,1,1,0,"s")
+        k_quant(0,1,0)
+        load_one_k(2,0,0)
+        k_cp(0,1,0,1,"s")
+        y_add(1,0,0,"g")
+        ln(2,1)
+        m_max(2,1)
+        k_pe(0,0,0,1)
+        k_cp(0,0,0,1,"s")
+        k_pe(0,0,0,0)
+        v_mm(3,0,1)
+        k_pe(0,0,1,1)
+        k_pe(0,0,1,0)
+        h_mm(1,1,0)
+        u_int(0,0,"s")
+        u_q(0,0)
         k_quant(0,1,1)
+        load_one_k(2,1,1)
+        v_mm(2,1,1)
+        k_cp(0,0,1,1,"s")
+        k_quant(0,0,1)
+        k_pe(2,1,0,0)
+        ln(3,0)
+        h_use(1,1,0)
+        k_cp(0,0,0,0,"s")
+        u_mul(2,1,0)
+        u_mul(2,1,1)
+        h_mm(0,1,1)
+        k_cp(2,1,0,0,"s")
+        k_cp(0,0,1,0,"s")
+        h_use(0,1,1)
+        k_quant(0,0,0)
+        m_max(3,0)
+        y_add(1,0,1,"g")
+        y_add(1,1,1,"g")
+        y_add(1,1,0,"g")
+        k_pe(2,0,1,1)
+        k_cp(2,0,1,1,"s")
+        k_pe(2,0,0,0)
+        h_mm(0,1,0)
+        h_use(0,1,0)
+        y_add(0,1,1,"g")
+        ln(3,1)
+        v_dv(2,1,0)
         k_pe(2,1,0,1)
         k_cp(2,1,0,1,"s")
         u_mul(3,0,1)
-        k_pe(2,0,1,1)
-        h_mm(1,1,0)
-        k_cp(2,0,1,1,"s")
-        h_use(1,1,0)
-        load_one_k(3,1,0)
-        v_dv(3,0,1)
-        y_add(0,0,1,"g")
-        ln(3,1)
-        load_one_k(2,0,0)
-        k_pe(2,0,0,0)
-        k_pe(2,0,0,1)
-        u_mul(3,0,0)
-        h_mm(0,1,0)
         k_cp(2,0,0,0,"s")
-        h_use(0,1,0)
-        k_cp(2,0,0,1,"s")
-        m_max(3,1)
+        u_int(2,0,"s")
+        k_pe(2,1,1,0)
+        v_dv(3,0,1)
+        h_mm(0,0,0)
+        h_use(0,0,0)
         k_pe(2,0,1,0)
         k_cp(2,0,1,0,"s")
+        k_pe(2,0,0,1)
+        k_cp(2,0,0,1,"s")
+        u_q(2,0)
+        m_max(3,1)
+        v_mm(3,0,0)
         k_quant(2,0,0)
-        k_pe(2,1,1,0)
-        k_pe(2,1,0,0)
-        k_quant(2,0,1)
-        v_mm(3,1,1)
-        k_cp(2,1,0,0,"s")
-        k_pe(2,1,1,1)
-        k_pe(3,1,0,0)
-        y_add(1,0,1,"g")
-        store(1,0,1)
         k_cp(2,1,1,0,"s")
+        k_pe(2,1,1,1)
+        k_pe(3,1,1,0)
         k_quant(2,1,0)
         k_cp(2,1,1,1,"s")
         k_quant(2,1,1)
-        h_mm(1,1,1)
-        h_use(1,1,1)
-        y_add(1,1,0,"g")
-        h_mm(0,1,1)
-        h_use(0,1,1)
+        h_mm(0,0,1)
+        k_quant(2,0,1)
         v_mm(3,1,0)
-        v_dv(3,1,0)
-        u_mul(3,1,0)
-        u_int(3,0,"s")
+        u_int(2,1,"s")
+        k_pe(3,1,0,0)
+        u_q(2,1)
+        v_dv(2,1,1)
+        h_use(0,0,1)
+        k_pe(3,1,1,1)
+        u_mul(3,0,0)
         h_mm(2,1,0)
         h_use(2,1,0)
-        u_mul(3,1,1)
-        v_dv(3,1,1)
-        k_pe(3,1,1,1)
-        v_dv(3,0,0)
-        h_mm(2,0,0)
-        h_use(2,0,0)
-        k_cp(3,1,0,0,"s")
-        y_add(0,1,0,"g")
-        u_q(3,0)
-        k_pe(3,1,0,1)
-        k_cp(3,1,0,1,"s")
-        k_pe(3,1,1,0)
-        y_add(1,1,1,"g")
-        k_cp(3,1,1,1,"s")
-        k_quant(3,1,1)
-        h_mm(2,1,1)
-        k_cp(3,1,1,0,"s")
-        y_add(0,1,1,"g")
-        store(1,0,0)
+        u_mul(3,1,0)
         load_one_k(3,0,0)
-        u_int(3,1,"s")
-        k_pe(3,0,0,0)
-        store(0,0,0)
-        store(1,1,1)
-        y_add(2,1,0,"g")
-        y_add(2,0,0,"g")
-        k_quant(3,1,0)
-        h_use(2,1,1)
-        k_cp(3,0,0,0,"s")
-        k_pe(3,0,1,0)
-        k_cp(3,0,1,0,"s")
-        store(2,0,0)
-        h_mm(2,0,1)
-        h_use(2,0,1)
-        k_pe(3,0,0,1)
-        k_pe(3,0,1,1)
-        u_q(3,1)
-        h_mm(3,1,1)
-        store(2,1,0)
-        k_cp(3,0,0,1,"s")
-        y_add(2,1,1,"v")
-        store(2,1,1)
-        k_quant(3,0,0)
-        store(0,0,1)
-        h_mm(3,1,0)
-        k_cp(3,0,1,1,"s")
-        k_quant(3,0,1)
-        h_mm(3,0,1)
-        y_add(2,0,1,"g")
-        h_use(3,1,1)
-        h_use(3,1,0)
-        y_add(3,1,0,"g")
-        y_add(3,1,1,"v")
-        h_use(3,0,1)
-        store(0,1,1)
+        v_mm(3,1,1)
+        u_mul(3,1,1)
         store(1,1,0)
+        h_mm(2,0,1)
+        y_add(0,1,0,"g")
+        h_use(2,0,1)
+        k_cp(3,1,1,1,"s")
+        k_pe(3,1,0,1)
+        k_pe(3,0,1,0)
+        k_cp(3,1,1,0,"s")
+        k_cp(3,1,0,0,"s")
+        h_mm(2,0,0)
+        k_quant(3,1,0)
+        h_use(2,0,0)
+        h_mm(2,1,1)
+        h_use(2,1,1)
+        u_int(3,0,"s")
+        store(0,1,1)
+        k_cp(3,1,0,1,"s")
+        u_q(3,0)
+        u_int(3,1,"s")
+        u_q(3,1)
+        y_add(0,0,0,"g")
+        k_quant(3,1,1)
+        k_cp(3,0,1,0,"s")
+        k_pe(3,0,0,0)
+        k_cp(3,0,0,0,"s")
+        k_pe(3,0,1,1)
+        k_cp(3,0,1,1,"s")
+        k_quant(3,0,0)
+        y_add(2,0,0,"v")
+        k_pe(3,0,0,1)
+        k_cp(3,0,0,1,"s")
+        k_quant(3,0,1)
+        h_mm(3,1,1)
+        h_use(3,1,1)
+        store(0,0,0)
+        y_add(0,0,1,"g")
+        store(1,0,0)
+        y_add(2,1,0,"g")
+        v_dv(3,1,1)
+        v_dv(3,1,0)
+        store(2,1,0)
+        store(1,1,1)
+        h_mm(3,0,1)
+        h_use(3,0,1)
+        v_dv(3,0,0)
+        y_add(2,0,1,"g")
         store(0,1,0)
+        y_add(2,1,1,"g")
+        y_add(3,1,1,"g")
         store(2,0,1)
         h_mm(3,0,0)
+        store(2,1,1)
+        store(0,0,1)
+        store(2,0,0)
         h_use(3,0,0)
-        y_add(3,0,1,"v")
+        y_add(3,0,1,"g")
+        h_mm(3,1,0)
+        h_use(3,1,0)
         store(3,1,1)
-        store(3,1,0)
+        store(1,0,1)
         store(3,0,1)
         y_add(3,0,0,"v")
         store(3,0,0)
+        y_add(3,1,0,"v")
+        store(3,1,0)

from contextlib import ExitStack

import concourse.mybir as mybir
from concourse.masks import make_identity

H, L, D, N = 4, 1024, 1024, 1024
C = N // H
FLOPS = 2 * 2 * L * D * N + 2 * H * L * L * C

F32 = mybir.dt.float32
BF16 = mybir.dt.bfloat16
U32 = mybir.dt.uint32
U8 = mybir.dt.uint8
FP8X4 = mybir.dt.float8_e4m3fn_x4
ACT = mybir.ActivationFunctionType
ALU = mybir.AluOpType

P = 128
PACK = 4
K_PASS = P * PACK
TINY = 2.0**-63


def tile_step_weighted_time_kernel_f4_kernel(
    tc, x, w_in, w_step, b_step, tau, kernel, alpha, h0, d, out
):
    nc = tc.nc

    with ExitStack() as ctx:
        raw_pool = ctx.enter_context(tc.tile_pool(name="raw", bufs=11))
        grp_pool = ctx.enter_context(tc.tile_pool(name="grp", bufs=5))
        keep = ctx.enter_context(tc.tile_pool(name="keep", bufs=1))
        kc_pool = ctx.enter_context(tc.tile_pool(name="kc", bufs=12))
        uc_pool = ctx.enter_context(tc.tile_pool(name="uc", bufs=8))
        ub_pool = ctx.enter_context(tc.tile_pool(name="ub", bufs=3))
        tr_psum = ctx.enter_context(tc.psum_pool(name="tr", bufs=3))
        acc_psum = ctx.enter_context(tc.psum_pool(name="acc", bufs=3))
        h_psum = ctx.enter_context(tc.psum_pool(name="hp", bufs=2))
        ctx.enter_context(tc.manual_schedule())

        dummy = keep.tile([P, 1], F32, name="dummy")
        nc.vector.memset(dummy[:], 0.0)
        rows = keep.tile([P, K_PASS], BF16, name="rows")
        vecs = keep.tile([P, N], BF16, name="vecs")
        nc.vector.memset(rows[:], 0.0)
        nc.vector.memset(vecs[:], 0.0)
        ident = keep.tile([P, P], F32, name="ident")
        make_identity(nc, ident[:])
        nc.scalar.dma_start(out=vecs[0:1, :], in_=b_step.unsqueeze(0))
        nc.scalar.dma_start(out=vecs[1:2, :], in_=h0.unsqueeze(0))
        nc.scalar.dma_start(out=vecs[2:3, :], in_=d.unsqueeze(0))
        nc.scalar.dma_start(out=rows[0:8, :], in_=alpha.rearrange("h (g q) -> (h g) q", q=K_PASS))
        nc.scalar.dma_start(out=rows[8:10, :], in_=tau.rearrange("(g q) -> g q", q=K_PASS))
        nc.scalar.activation(out=dummy[:], in_=dummy[:], func=ACT.Sigmoid)

        ident_b = keep.tile([P, P], BF16, name="ident_b")
        nc.vector.tensor_copy(out=ident_b[:], in_=ident[:])

        def load_rows(src, g, half):
            raw = raw_pool.tile([P, 2, 1024], BF16, name="raw", align_bytes=64)
            view = src[g * K_PASS : (g + 1) * K_PASS, :].rearrange("(m t) k -> m t k", t=PACK)
            nc.sync.dma_start(out=raw[:], in_=view[:, 2 * half : 2 * half + 2, :])
            return raw

        def load_w_part(w, kp, c0):
            raw = raw_pool.tile([P, PACK, 256], BF16, name="raw", align_bytes=64)
            view = w[kp * K_PASS : (kp + 1) * K_PASS, c0 : c0 + 256]
            nc.sync.dma_start(out=raw[:], in_=view.rearrange("(p j) n -> p j n", j=PACK))
            return raw

        def load_w(w, nh, kp):
            raw = raw_pool.tile([P, PACK, 512], BF16, name="raw", align_bytes=64)
            view = w[kp * K_PASS : (kp + 1) * K_PASS, nh * 512 : (nh + 1) * 512]
            nc.sync.dma_start(out=raw[:], in_=view.rearrange("(p j) n -> p j n", j=PACK))
            return raw

        def copy(eng, out_ap, in_ap):
            if eng == "s":
                nc.scalar.copy(out_ap, in_ap)
            elif eng == "v":
                nc.vector.tensor_copy(out=out_ap, in_=in_ap)
            else:
                nc.gpsimd.tensor_scalar(
                    out=out_ap, in0=in_ap, scalar1=1.0, scalar2=0.0, op0=ALU.mult, op1=ALU.add
                )

        def t_pe(key, raw, half, kp):
            words = raw[:].rearrange("p t k -> p (t k)").bitcast(F32)
            bank = tr_psum.tile([P, 2, 2, P], F32, name="bank")
            for tt in range(2):
                for u in range(2):
                    first = tt * 512 + 256 * kp + u
                    nc.tensor.transpose(
                        bank[:, tt, u, :], words[:, first : tt * 512 + 256 * (kp + 1) : 2], ident[:]
                    )
            tbank[key, half, kp] = bank

        def t_cp(key, half, kp, eng):
            if (key, kp) not in groups_of:
                grp = grp_pool.tile([P, 2048], BF16, name="grp", align_bytes=64)
                groups_of[key, kp] = grp
            dst = groups_of[key, kp][:].bitcast(F32)[:, 512 * half : 512 * (half + 1)]
            copy(
                eng,
                dst.rearrange("p (t r u) -> p t r u", t=2, u=2),
                tbank[key, half, kp][:].rearrange("p t u r -> p t r u"),
            )

        def quantize(grp, pool, name):
            width = grp.shape[1] // PACK
            codes = pool.tile([P, width], U32, name=name + "_c", align_bytes=64)
            scales = pool.tile([P, width], U8, name=name + "_s", align_bytes=64)
            nc.vector.quantize_mx(out=codes[:].bitcast(FP8X4), scales=scales[:], in_=grp[:])
            return codes, scales

        def interleave(eng, dst, raw):
            if eng == "g":
                copy(eng, dst.rearrange("p (c t) -> p c t", t=PACK), raw[:].rearrange("p t c -> p c t"))
            else:
                copy(
                    eng,
                    dst.rearrange("p (c i t) -> p c t i", i=4, t=PACK),
                    raw[:].rearrange("p t (c i) -> p c t i", i=4),
                )

        def quantize_half(grp, half, planes):
            cols = slice(256 * half, 256 * (half + 1))
            nc.vector.quantize_mx(
                out=planes[0][:, cols].bitcast(FP8X4),
                scales=planes[1][:, cols],
                in_=grp[:, 1024 * half : 1024 * (half + 1)],
            )

        def new_planes(pool, name):
            codes = pool.tile([P, 512], U32, name=name + "_c", align_bytes=64)
            scales = pool.tile([P, 512], U8, name=name + "_s", align_bytes=64)
            return codes, scales

        def prep_w(raw, eng, name):
            grp = grp_pool.tile([P, 2048], BF16, name="grp", align_bytes=64)
            interleave(eng, grp[:], raw)
            return quantize(grp, keep, name)

        def mx(out_ap, stat, c0, mov, n0, width, start, stop):
            nc.tensor.matmul_mx(
                out=out_ap,
                lhsT=stat[0][:, c0 : c0 + P].bitcast(FP8X4),
                lhsT_scale=stat[1][:, c0 : c0 + P],
                rhs=mov[0][:, n0 : n0 + width].bitcast(FP8X4),
                rhs_scale=mov[1][:, n0 : n0 + width],
                start=start,
                stop=stop,
            )

        rx = {}
        rw = {}
        rk = {}

        def load_x(g):
            for half in range(2):
                rx[g, half] = load_rows(x, g, half)

        def load_ws(w, tag, nh):
            for kp in range(2):
                rw[tag, nh, kp] = load_w(w, nh, kp)

        def load_one_k(j, g, half):
            rk[j, g, half] = load_rows(kernel[j], g, half)

        def load_one_x(g, half):
            rx[g, half] = load_rows(x, g, half)

        def load_one_w(w, tag, nh, kp):
            rw[tag, nh, kp] = load_w(w, nh, kp)

        def load_k(j):
            for g in range(2):
                for half in range(2):
                    rk[j, g, half] = load_rows(kernel[j], g, half)

        sm = keep.tile([P, PACK, 10], F32, name="sm")
        bc = keep.tile([P, 3, N], BF16, name="bc")

        def cols_pe():
            bank = tr_psum.tile([P, PACK, P], BF16, name="bank")
            for t in range(PACK):
                nc.tensor.transpose(bank[:, t, :], rows[:, t : K_PASS : PACK], ident_b[:])
            tbank["cols"] = bank

        def cols_cp():
            nc.vector.tensor_copy(out=sm[:], in_=tbank["cols"][:, :, 0:10])

        def spread_pe(r):
            bank = acc_psum.tile([P, N], BF16, name="acc")
            for nh in range(2):
                nc.tensor.matmul(
                    bank[:, nh * 512 : (nh + 1) * 512],
                    lhsT=ident_b[:, r : r + 1].to_broadcast([P, P]),
                    rhs=vecs[:, nh * 512 : (nh + 1) * 512],
                    start=True,
                    stop=True,
                )
            tbank["spread", r] = bank

        def spread_cp(r, eng):
            copy(eng, bc[:, r, :], tbank["spread", r][:])

        groups_of = {}
        tbank = {}
        qx = {}
        qw = {}
        qk = {}
        qu = {}
        a = {}
        sg = {}
        for lg in range(2):
            for nh in range(2):
                a[lg, nh] = keep.tile([P, PACK, 512], F32, name="a%d%d" % (lg, nh))
                sg[lg, nh] = keep.tile([P, PACK, 512], F32, name="sg%d%d" % (lg, nh))

        def g_mm(lg, nh, t):
            acc = acc_psum.tile([P, 512], F32, name="acc")
            for kp in range(2):
                mx(acc[:], qx[lg, kp], t * P, qw["s", nh, kp], 0, 512, kp == 0, kp == 1)
            gacc[lg, nh, t] = acc

        def g_use(lg, nh, t):
            acc = gacc[lg, nh, t]
            nc.vector.tensor_tensor(
                out=a[lg, nh][:, t, :], in0=acc[:], in1=bc[:, 0, nh * 512 : (nh + 1) * 512], op=ALU.add
            )

        def sig(lg, nh, tp):
            pair = slice(2 * tp, 2 * tp + 2)
            nc.scalar.activation(
                out=sg[lg, nh][:, pair, :], in_=a[lg, nh][:, pair, :], func=ACT.Sigmoid, scale=-1.0
            )

        def cols_of(j):
            return slice((j % 2) * C, (j % 2 + 1) * C)

        def ln(j, lg):
            s = sg[lg, j // 2][:, :, cols_of(j)]
            nc.scalar.activation(out=s, in_=s, func=ACT.Ln, bias=TINY)

        def m_max(j, lg):
            m = sg[lg, j // 2][:, :, cols_of(j)]
            av = a[lg, j // 2][:, :, cols_of(j)]
            nc.vector.scalar_tensor_tensor(out=m, in0=m, scalar=-1.0, in1=av, op0=ALU.mult, op1=ALU.max)

        vacc = {}
        gacc = {}
        ub_of = {}
        ug_of = {}
        hacc = {}

        def v_mm(j, lg, tp):
            acc = acc_psum.tile([P, 2, C], F32, name="acc")
            for tt in range(2):
                for kp in range(2):
                    mx(acc[:, tt, :], qx[lg, kp], (2 * tp + tt) * P, qw["i", j // 2, kp], (j % 2) * C, C, kp == 0, kp == 1)
            vacc[j, lg, tp] = acc

        def u_mul(j, lg, tp):
            acc = vacc[j, lg, tp]
            if (j, lg) not in ub_of:
                ub = ub_pool.tile([P, PACK, C], BF16, name="ub", align_bytes=64)
                ub_of[j, lg] = ub
            m = sg[lg, j // 2][:, :, cols_of(j)]
            for tt in range(2):
                t = 2 * tp + tt
                nc.vector.scalar_tensor_tensor(
                    out=ub_of[j, lg][:, t, :],
                    in0=m[:, t, :],
                    scalar=sm[:, t, 8 + lg : 9 + lg],
                    in1=acc[:, tt, :],
                    op0=ALU.mult,
                    op1=ALU.mult,
                )

        def v_dv(j, lg, tp):
            nc.vector.tensor_tensor(
                out=a[lg, j // 2][:, 2 * tp : 2 * tp + 2, cols_of(j)],
                in0=vacc[j, lg, tp][:],
                in1=bc[:, 2, j * C : (j + 1) * C].unsqueeze(1).to_broadcast([P, 2, C]),
                op=ALU.mult,
            )

        def u_int(j, lg, eng):
            ug = ub_pool.tile([P, C * PACK], BF16, name="ug", align_bytes=64)
            interleave(eng, ug[:], ub_of[j, lg])
            ug_of[j, lg] = ug

        def u_q(j, lg):
            qu[j, lg] = quantize(ug_of[j, lg], uc_pool, "qu")

        def h_mm(j, g, tp):
            hp = h_psum.tile([P, 2, C], F32, name="hp")
            for tt in range(2):
                for kp in range(2):
                    mx(hp[:, tt, :], qk[j, g, kp], (2 * tp + tt) * P, qu[j, kp], 0, C, kp == 0, kp == 1)
            hacc[j, g, tp] = hp

        def h_use(j, g, tp):
            hp = hacc[j, g, tp]
            y = sg[g, j // 2][:, :, cols_of(j)]
            for tt in range(2):
                t = 2 * tp + tt
                nc.vector.scalar_tensor_tensor(
                    out=y[:, t, :],
                    in0=bc[:, 1, j * C : (j + 1) * C],
                    scalar=sm[:, t, 2 * j + g : 2 * j + g + 1],
                    in1=hp[:, tt, :],
                    op0=ALU.mult,
                    op1=ALU.add,
                )

        def y_add(j, g, tp, eng):
            y = sg[g, j // 2][:, 2 * tp : 2 * tp + 2, cols_of(j)]
            dv = a[g, j // 2][:, 2 * tp : 2 * tp + 2, cols_of(j)]
            e = nc.gpsimd if eng == "g" else nc.vector
            e.tensor_tensor(out=y, in0=y, in1=dv, op=ALU.add)

        def store(j, g, tp):
            view = out[g * K_PASS : (g + 1) * K_PASS, j * C : (j + 1) * C].rearrange("(m t) c -> m t c", t=PACK)
            nc.sync.dma_start(
                out=view[:, 2 * tp : 2 * tp + 2, :], in_=sg[g, j // 2][:, 2 * tp : 2 * tp + 2, cols_of(j)]
            )

        def k_pe(j, g, half, kp):
            t_pe((j, g), rk[j, g, half], half, kp)

        def k_cp(j, g, half, kp, eng):
            t_cp((j, g), half, kp, eng)

        def k_quant(j, g, kp):
            qk[j, g, kp] = quantize(groups_of[(j, g), kp], kc_pool, "qk")

        def x_pe(g, half, kp):
            t_pe(("x", g), rx[g, half], half, kp)

        def x_cp(g, half, kp, eng):
            t_cp(("x", g), half, kp, eng)

        for g in range(2):
            for kp in range(2):
                qx[g, kp] = new_planes(keep, "qx%d%d" % (g, kp))
                if g == 0:
                    qw["s", 0, kp] = new_planes(keep, "qws0%d" % kp)

        wgrp = {}

        def x_quant(g, kp, half):
            quantize_half(groups_of[("x", g), kp], half, qx[g, kp])

        def load_first(kp, half):
            rw["s", 0, kp, half] = load_w_part(w_step, kp, 256 * half)

        def first_int(kp, half, eng):
            if ("s", 0, kp) not in wgrp:
                grp = grp_pool.tile([P, 2048], BF16, name="grp", align_bytes=64)
                wgrp["s", 0, kp] = grp
            interleave(eng, wgrp["s", 0, kp][:, 1024 * half : 1024 * (half + 1)], rw["s", 0, kp, half])

        def first_quant(kp, half):
            quantize_half(wgrp["s", 0, kp], half, qw["s", 0, kp])

        def w_int(tag, nh, kp, eng):
            grp = grp_pool.tile([P, 2048], BF16, name="grp", align_bytes=64)
            interleave(eng, grp[:], rw[tag, nh, kp])
            wgrp[tag, nh, kp] = grp

        def w_quant(tag, nh, kp):
            qw[tag, nh, kp] = quantize(wgrp[tag, nh, kp], keep, "qw%s%d%d" % (tag, nh, kp))

        load_one_x(1,0)
        load_first(1,0)
        first_int(1,0,"v")
        load_first(0,1)
        x_pe(1,0,1)
        x_cp(1,0,1,"s")
        load_one_x(1,1)
        x_pe(1,0,0)
        first_int(0,1,"v")
        load_first(1,1)
        x_cp(1,0,0,"s")
        load_one_w(w_step,"s",1,1)
        x_pe(1,1,1)
        load_one_x(0,0)
        load_first(0,0)
        load_one_x(0,1)
        load_one_w(w_in,"i",1,1)
        x_quant(1,1,0)
        x_cp(1,1,1,"s")
        first_quant(0,1)
        spread_pe(0)
        spread_cp(0,"s")
        x_pe(1,1,0)
        x_quant(1,0,0)
        load_one_w(w_step,"s",1,0)
        spread_pe(2)
        load_one_w(w_in,"i",0,1)
        first_quant(1,0)
        load_one_k(2,0,1)
        x_cp(1,1,0,"s")
        spread_cp(2,"s")
        x_pe(0,0,1)
        first_int(1,1,"v")
        first_quant(1,1)
        load_one_k(1,0,0)
        w_int("s",1,1,"v")
        x_cp(0,0,1,"s")
        x_quant(1,1,1)
        x_pe(0,0,0)
        x_cp(0,0,0,"s")
        w_quant("s",1,1)
        first_int(0,0,"v")
        first_quant(0,0)
        x_quant(1,0,1)
        x_quant(0,1,0)
        x_pe(0,1,0)
        load_one_w(w_in,"i",1,0)
        x_cp(0,1,0,"s")
        w_int("i",1,1,"s")
        x_quant(0,0,0)
        x_pe(0,1,1)
        w_int("s",1,0,"s")
        x_cp(0,1,1,"v")
        g_mm(1,0,3)
        x_quant(0,0,1)
        load_one_w(w_in,"i",0,0)
        x_quant(0,1,1)
        g_mm(0,0,1)
        g_use(1,0,3)
        g_mm(0,0,0)
        g_use(0,0,1)
        g_use(0,0,0)
        load_one_k(3,1,1)
        g_mm(1,0,0)
        g_use(1,0,0)
        g_mm(1,0,2)
        g_use(1,0,2)
        g_mm(1,0,1)
        g_use(1,0,1)
        g_mm(0,0,3)
        g_use(0,0,3)
        w_int("i",0,1,"g")
        cols_pe()
        cols_cp()
        sig(0,0,0)
        w_quant("s",1,0)
        sig(1,0,0)
        w_quant("i",0,1)
        w_quant("i",1,1)
        g_mm(0,0,2)
        g_use(0,0,2)
        g_mm(0,1,0)
        g_use(0,1,0)
        g_mm(1,1,0)
        g_use(1,1,0)
        g_mm(0,1,1)
        g_use(0,1,1)
        g_mm(1,1,2)
        g_mm(1,1,3)
        g_use(1,1,2)
        load_one_k(3,0,1)
        w_int("i",0,0,"g")
        sig(1,0,1)
        g_mm(0,1,3)
        g_use(1,1,3)
        g_use(0,1,3)
        load_one_k(0,0,0)
        g_mm(0,1,2)
        w_quant("i",0,0)
        g_use(0,1,2)
        sig(0,0,1)
        ln(1,1)
        g_mm(1,1,1)
        g_use(1,1,1)
        m_max(1,1)
        v_mm(1,1,1)
        k_pe(1,0,0,1)
        ln(0,1)
        m_max(0,1)
        v_mm(1,1,0)
        v_dv(1,1,0)
        load_one_k(1,0,1)
        u_mul(1,1,1)
        u_mul(1,1,0)
        k_pe(1,0,1,1)
        k_pe(1,0,1,0)
        v_mm(1,0,1)
        k_pe(1,0,0,0)
        load_one_k(0,1,0)
        ln(1,0)
        load_one_k(1,1,1)
        k_pe(1,1,1,1)
        ln(0,0)
        load_one_k(0,0,1)
        m_max(1,0)
        m_max(0,0)
        k_cp(1,0,1,0,"s")
        v_dv(1,1,1)
        u_mul(1,0,1)
        v_dv(1,0,1)
        v_mm(0,0,1)
        u_mul(0,0,1)
        v_dv(0,0,1)
        v_mm(0,1,0)
        u_mul(0,1,0)
        v_dv(0,1,0)
        u_int(1,1,"g")
        k_pe(1,1,1,0)
        load_one_k(0,1,1)
        k_cp(1,0,1,1,"s")
        v_mm(1,0,0)
        v_dv(1,0,0)
        k_cp(1,0,0,1,"s")
        v_mm(0,1,1)
        v_dv(0,1,1)
        u_mul(1,0,0)
        w_int("i",1,0,"g")
        w_quant("i",1,0)
        u_mul(0,1,1)
        sig(0,1,0)
        u_int(1,0,"g")
        sig(1,1,0)
        v_mm(0,0,0)
        u_mul(0,0,0)
        v_dv(0,0,0)
        k_pe(0,1,0,0)
        load_one_k(2,1,0)
        load_one_k(1,1,0)
        u_q(1,1)
        k_cp(1,1,1,1,"s")
        sig(0,1,1)
        k_pe(1,1,0,0)
        k_pe(1,1,0,1)
        k_cp(1,0,0,0,"s")
        k_quant(1,0,0)
        v_mm(2,1,0)
        u_q(1,0)
        k_quant(1,0,1)
        spread_pe(1)
        sig(1,1,1)
        k_pe(0,1,1,1)
        v_mm(2,0,1)
        k_cp(1,1,1,0,"s")
        k_cp(1,1,0,0,"s")
        ln(2,0)
        k_quant(1,1,0)
        m_max(2,0)
        k_cp(1,1,0,1,"s")
        k_quant(1,1,1)
        h_mm(1,0,1)
        h_mm(1,0,0)
        load_one_k(3,1,0)
        spread_cp(1,"s")
        h_use(1,0,0)
        v_mm(2,0,0)
        u_mul(2,0,0)
        h_use(1,0,1)
        v_dv(2,0,0)
        k_cp(0,1,0,0,"s")
        u_mul(2,0,1)
        v_dv(2,0,1)
        k_pe(0,1,0,1)
        k_pe(0,1,1,0)
        h_mm(1,1,1)
        h_use(1,1,1)
        k_cp(0,1,1,1,"s")
        u_int(0,1,"s")
        u_q(0,1)
        k_cp(0,1,1,0,"s")
        k_quant(0,1,0)
        load_one_k(2,0,0)
        k_cp(0,1,0,1,"s")
        y_add(1,0,0,"g")
        ln(2,1)
        m_max(2,1)
        k_pe(0,0,0,1)
        k_cp(0,0,0,1,"s")
        k_pe(0,0,0,0)
        v_mm(3,0,1)
        k_pe(0,0,1,1)
        k_pe(0,0,1,0)
        h_mm(1,1,0)
        u_int(0,0,"s")
        u_q(0,0)
        k_quant(0,1,1)
        load_one_k(2,1,1)
        v_mm(2,1,1)
        k_cp(0,0,1,1,"s")
        k_quant(0,0,1)
        k_pe(2,1,0,0)
        ln(3,0)
        h_use(1,1,0)
        k_cp(0,0,0,0,"s")
        u_mul(2,1,0)
        u_mul(2,1,1)
        h_mm(0,1,1)
        k_cp(2,1,0,0,"s")
        k_cp(0,0,1,0,"s")
        h_use(0,1,1)
        k_quant(0,0,0)
        m_max(3,0)
        y_add(1,0,1,"g")
        y_add(1,1,1,"g")
        y_add(1,1,0,"g")
        k_pe(2,0,1,1)
        k_cp(2,0,1,1,"s")
        k_pe(2,0,0,0)
        h_mm(0,1,0)
        h_use(0,1,0)
        y_add(0,1,1,"g")
        ln(3,1)
        v_dv(2,1,0)
        k_pe(2,1,0,1)
        k_cp(2,1,0,1,"s")
        u_mul(3,0,1)
        k_cp(2,0,0,0,"s")
        u_int(2,0,"s")
        k_pe(2,1,1,0)
        v_dv(3,0,1)
        h_mm(0,0,0)
        h_use(0,0,0)
        k_pe(2,0,1,0)
        k_cp(2,0,1,0,"s")
        k_pe(2,0,0,1)
        k_cp(2,0,0,1,"s")
        u_q(2,0)
        m_max(3,1)
        v_mm(3,0,0)
        k_quant(2,0,0)
        k_cp(2,1,1,0,"s")
        k_pe(2,1,1,1)
        k_pe(3,1,1,0)
        k_quant(2,1,0)
        k_cp(2,1,1,1,"s")
        k_quant(2,1,1)
        h_mm(0,0,1)
        k_quant(2,0,1)
        v_mm(3,1,0)
        u_int(2,1,"s")
        k_pe(3,1,0,0)
        u_q(2,1)
        v_dv(2,1,1)
        h_use(0,0,1)
        k_pe(3,1,1,1)
        u_mul(3,0,0)
        h_mm(2,1,0)
        h_use(2,1,0)
        u_mul(3,1,0)
        load_one_k(3,0,0)
        v_mm(3,1,1)
        u_mul(3,1,1)
        store(1,1,0)
        h_mm(2,0,1)
        y_add(0,1,0,"g")
        h_use(2,0,1)
        k_cp(3,1,1,1,"s")
        k_pe(3,1,0,1)
        k_pe(3,0,1,0)
        k_cp(3,1,1,0,"s")
        k_cp(3,1,0,0,"s")
        h_mm(2,0,0)
        k_quant(3,1,0)
        h_use(2,0,0)
        h_mm(2,1,1)
        h_use(2,1,1)
        u_int(3,0,"s")
        store(0,1,1)
        k_cp(3,1,0,1,"s")
        u_q(3,0)
        u_int(3,1,"s")
        u_q(3,1)
        y_add(0,0,0,"g")
        k_quant(3,1,1)
        k_cp(3,0,1,0,"s")
        k_pe(3,0,0,0)
        k_cp(3,0,0,0,"s")
        k_pe(3,0,1,1)
        k_cp(3,0,1,1,"s")
        k_quant(3,0,0)
        y_add(2,0,0,"v")
        k_pe(3,0,0,1)
        k_cp(3,0,0,1,"s")
        k_quant(3,0,1)
        h_mm(3,1,1)
        h_use(3,1,1)
        store(0,0,0)
        y_add(0,0,1,"g")
        store(1,0,0)
        y_add(2,1,0,"g")
        v_dv(3,1,1)
        v_dv(3,1,0)
        store(2,1,0)
        store(1,1,1)
        h_mm(3,0,1)
        h_use(3,0,1)
        v_dv(3,0,0)
        y_add(2,0,1,"g")
        store(0,1,0)
        y_add(2,1,1,"g")
        y_add(3,1,1,"g")
        store(2,0,1)
        h_mm(3,0,0)
        store(2,1,1)
        store(0,0,1)
        store(2,0,0)
        h_use(3,0,0)
        y_add(3,0,1,"g")
        h_mm(3,1,0)
        h_use(3,1,0)
        store(3,1,1)
        store(1,0,1)
        store(3,0,1)
        y_add(3,0,0,"v")
        store(3,0,0)
        y_add(3,1,0,"v")
        store(3,1,0)
